import numpy as np, ml_dtypes
CORES = [3,11,19,27,35,43,51,59]
N = 8
import mx_ref
BF = ml_dtypes.bfloat16
def gentries(a):
    return np.ascontiguousarray(a.reshape(8, 16, -1).transpose(0, 2, 1)).reshape(8, -1)
def gtable(e):
    e = np.asarray(e); return np.ascontiguousarray(e.reshape(8, -1, 16).transpose(0, 2, 1)).reshape(128, -1).astype(np.int32)
def gcols(t, e):
    v = np.concatenate([t.reshape(8, 16, -1, 4), np.zeros((8, 16, 1, 4), BF)], axis=2)
    return np.ascontiguousarray(np.stack([v[g][:, e[g]] for g in range(8)])).reshape(128, -1)
def tile(rs):
    return np.stack(rs, axis=2).reshape(128, -1).astype(BF)
def pick(q, e):
    c = np.concatenate([q[0].reshape(128, -1, 4), np.zeros((128, 1, 4), np.uint8)], axis=1); s = np.concatenate([q[1], np.ones((16, 1), np.uint8)], axis=1)
    return (np.ascontiguousarray(c[:, e].reshape(128, -1)), np.ascontiguousarray(s[:, e]))
def join(*qs):
    return (np.concatenate([q[0] for q in qs], axis=1), np.concatenate([q[1] for q in qs], axis=1))
def put(q, e, v):
    c, s = q[0].reshape(128, -1, 4).copy(), q[1].copy(); c[:, e] = v[0].reshape(128, -1, 4); s[:, e] = v[1]
    return (c.reshape(128, -1), s)
def pk(c, s):
    return (np.ascontiguousarray(c), mx_ref.live(s))
def emit(q):
    return q[0], q[1]
def packed(v, rng):
    q = [mx_ref.quantize(np.ascontiguousarray(v[r])) for r in range(N)]
    return np.stack([a for a, b in q]), np.stack([mx_ref.plane(b, rng) for a, b in q])
def values_of_codes():
    e, c = np.zeros((128, 128, 4), np.float32), np.zeros((128, 2, 4), np.uint8)
    e[np.arange(128), np.arange(128), 0] = 1
    c[:127, :, 0] = np.arange(256).reshape(2, 128).T[:127]
    return mx_ref.matmul(mx_ref.quantize(e.reshape(128, 512).astype(BF)), (c.reshape(128, 8), np.full((16, 2), 127, np.uint8))).T.reshape(-1).astype(np.float64)
CODE_VALUE, SCALE_VALUE = values_of_codes(), 2.0 ** (np.arange(256) - 127.0)
def decode(q):
    return (CODE_VALUE[q[0]].reshape(16, 8, -1, 4) * SCALE_VALUE[q[1]][:, None, :, None] + 0.0).reshape(128, -1).astype(np.float32)
def f(rng, *shape):
    return mx_ref.flush((rng.standard_normal(shape, dtype=np.float32) * np.exp2(rng.integers(-2, 3, shape[:-1] + (1,)))).astype(BF))
def wide(rng, *shape, cols=0):
    v = rng.standard_normal(shape, dtype=np.float32) * np.exp2(rng.integers(-12, 13, shape)).astype(np.float32)
    if cols: v *= np.repeat(np.exp2(rng.integers(-cols, cols + 1, shape[:-2] + (1, shape[-1] // 4))) * (rng.random(shape[:-2] + (1, shape[-1] // 4)) > 0.0625), 4, axis=-1).astype(np.float32)
    return mx_ref.flush(v.astype(BF))
C, DOUBLINGS = 320, 9
STEP = [1, 2, 4]
def numbers_of(rng):
    return {"x": np.array(f(rng, N, 128, 4 * C)), "u": np.array(f(rng, N, 128, 512)), "v": np.array(f(rng, N, 128, 512))}
def links(rng, far=False):
    l = rng.permuted(np.tile(np.arange(C), (N, 8, 2, 1)), axis=3)
    if far:
        for r in range(N):
            for i, g in enumerate(rng.permutation(8)[:6]):
                o = rng.permutation(C)
                l[r, g, 0, o] = np.append(o[1:], o[[0, C - 1, C // 2][i % 3]])
                if i < 3: l[r, g, 1] = l[r, g, 0]
    return l
def stored(l):
    return {"la": np.stack([gtable(l[r, :, 0]) for r in range(N)]), "lb": np.stack([gtable(l[r, :, 1]) for r in range(N)])}
def layers(rng, still=[]):
    w = np.array(f(rng, N, 128, 2048)).reshape(N, 8, 16, 4, 8, 16, 4)
    for i in still:
        w[:, :, i] = 0
        w[:, :, :, :, :, i] = 0
    return w
def weights(rng, w):
    c, p = packed(np.ascontiguousarray(w).reshape(N, 128, 2048), rng)
    return {"wc": c, "ws": p}
def setup_inputs(rng):
    return {**numbers_of(rng), **stored(links(rng)), **weights(rng, layers(rng))}
def setup_inputs_ties(rng):
    d = numbers_of(rng)
    o = rng.permutation(N)
    k = rng.integers(-2, 3, (N, 8, C))
    k[o[1]] = -rng.integers(1, 5, (8, C))
    far = rng.permutation(8)
    k[o[2], far[:4]] = 1
    k[o[3], rng.permutation(8)[:4]] = -1
    l = links(rng, True)
    way = rng.permutation(C)
    way[-2:] = np.sort(way[-2:])
    for g, end, top in ((far[4], way[-1], way[-1]), (far[5], way[0], 0)):
        l[o[2], g, 0, way] = np.append(way[1:], end)
        l[o[2], g, 1] = np.arange(C)
        k[o[2], g] = 1
        k[o[2], g, top] = 2
    x = d["x"].reshape(N, 8, 16, C, 4)
    x[:, :, 0] = 0
    x[:, :, 0, :, 0] = k.astype(np.float32).astype(BF)
    u = d["u"].reshape(N, 128, 128, 4)
    u[:, :, ::16] = 0
    for r in range(N):
        for h in range(0, 128, 16): u[r, h, h, 0] = 0.0 if r == o[0] else 1.0
    return {"x": x.reshape(N, 128, 4 * C), "u": u.reshape(N, 128, 512), "v": d["v"], **stored(l), **weights(rng, layers(rng, [0]))}
def setup_inputs_near(rng):
    d = numbers_of(rng)
    x = d["x"].astype(np.float32).reshape(N, 8, 16, C, 4)
    x[:, :, 0] = 0
    x[:, :, 8:] = 0
    u = d["u"].reshape(N, 128, 128, 4)
    u[:, :, ::16] = 0
    w = layers(rng, [0, 8, 9, 10, 11, 12, 13, 14, 15])
    o = rng.permutation(N) % 4
    for r in range(N):
        s = rng.integers(0, 16, (8, C))
        digits = ((s[:, :, None] >> np.arange(4)) & 1) * np.exp2(np.arange(4) - 23.0)
        if o[r] < 3: x[r, :, 12, :, 0] = rng.choice([-1.0, 1.0], (8, C)) * 2.0 ** -20
        if o[r] < 2:
            x[r, :, 0, :, 0] = np.where(rng.permutation(8) < 4, -1.0, 1.0)[:, None]
            x[r, :, 8] = digits
            x[r, :, 11, :, 0] = 2.0 ** -10
        elif o[r] == 2: x[r, :, 8] = digits * rng.choice([-1.0, 1.0], (8, C, 1))
        else:
            e = rng.integers(-1, 2, (8, C)) * 2.0 ** -30
            x[r, :, 8, :, 0] = 1.25 * e
            x[r, :, 9, :, 0] = -1.125 * e
            x[r, :, 15, :, 0] = 2.0 ** -30
            for g in range(8):
                w[r, g, 12, 0, g, 10, 0] = 2.0 ** -18
                w[r, g, 14, 0, g, 10, 0] = 2.0 ** -8
        at = [0, C - 1, int(rng.integers(C)), int(rng.integers(C))]
        for g, j in zip(rng.permutation(8)[:4], at): x[r, g, 0, j, 0] = 2.0 ** 29 * rng.choice([-1.0, 1.0])
        k = 1.0 if o[r] == 0 else 2.0 ** -30
        for h in range(0, 128, 16):
            u[r, h, h, 0] = k if o[r] < 2 else 1.0
            if o[r] < 2: u[r, h + 11, h, 0] = k
            if o[r] < 3: u[r, h + 8, h] = k
            else:
                u[r, h + 8, h, 0] = k
                u[r, h + 9, h, 0] = 1.125 * k
                u[r, h + 10, h, 0] = k
    return {"x": x.reshape(N, 128, 4 * C).astype(BF), "u": u.reshape(N, 128, 512), "v": d["v"], **stored(links(rng, True)), **weights(rng, w)}
def setup_inputs_odd(rng):
    d = numbers_of(rng)
    x = (1.0 + (2 * rng.integers(0, 64, (N, 16, 8, C, 4)) + 1) * 2.0 ** -7) * np.exp2(-rng.integers(0, 7, (N, 16, 8, C, 4)).astype(np.float64)) * rng.choice([-1.0, 1.0], (N, 16, 8, C, 4))
    x[:, :, 0, :, 0] = np.where(rng.random((N, 16, C)) < 0.25, 1.875, 1.96875) * 2.0 ** 8
    x[:, ::2, 1, :, 0] = rng.choice([-1.0, 1.0], (N, 8, C)) * (8 + rng.integers(0, 2, (N, 8, C))) * 2.0 ** -8
    u = d["u"].reshape(N, 16, 8, 128, 4)
    u[:, :, :, ::16] = 0
    for g in range(8): u[:, 2 * g, 1, 16 * g, 0] = 1.0
    return {"x": x.astype(np.float32).reshape(N, 128, 4 * C).astype(BF), "u": u.reshape(N, 128, 512), "v": d["v"], **stored(links(rng)), **weights(rng, layers(rng, [0, 8]))}
def setup_inputs_ends(rng):
    d = numbers_of(rng)
    o, e = rng.permutation(N) % 4, rng.permutation(N) % 4
    m = int(rng.integers(8))
    l = links(rng, True)
    small = -(1.0 + 0.125 * rng.integers(0, 8, (N, 8, 16, C, 4)))
    x = -(0.88 + 0.08 * rng.random((N, 8, 16, C, 4))) * 2.0 ** 30
    x[o == 1] *= rng.choice([-1.0, 1.0], (N, 1, 1, C, 1))[o == 1]
    x[o == 2] = small[o == 2] * 2.0 ** -30
    x[o == 3] = d["x"].astype(np.float32).reshape(N, 8, 16, C, 4)[o == 3][:, :, :, :1]
    x[:, m] = small[:, m] * 2.0 ** -20
    u = d["u"].astype(np.float32).reshape(N, 8, 16, 128, 4)
    v = rng.choice([-1.0, 1.0], (N, 128, 512)) * np.where(o < 2, 2.0 ** 30, 2.0 ** -30)[:, None, None]
    w = np.zeros((N, 128, 4, 128, 4), np.float32)
    i = np.arange(128)
    for r in range(N):
        h = rng.permutation(8)
        c = np.where(h < 2, 0.0, h % 2 * 2.0 - 1.0)[:, None]
        if o[r] < 2: u[r, :, :, ::16] = c * (0.9 + 0.1 * rng.random((8, 16, 8, 4))) * 2.0 ** 30
        if o[r] == 2: u[r, :, :, ::16] = c * (1.0 + 0.125 * rng.integers(0, 8, (8, 16, 8, 4))) * 2.0 ** -30
        if o[r] == 3: u[r, :, :, ::16] *= np.abs(c).astype(np.float32)
        k = np.zeros(8)
        if o[r] < 2: k = rng.choice([-1.0, 1.0], 8) * np.array([0.75, 0.5, 2.0 ** -8])[rng.permutation(8) % 3]
        k[m] = 2.0 ** 8
        for b in range(4): w[r, i, b, i, b] = k[i // 16]
        if e[r] < 2:
            l[r, :, e[r]] = C - 1
            l[r, :, 1 - e[r]] = 0
        if e[r] == 2: l[r] = rng.integers(0, C, (8, 2, C))
    u[:, m, :, ::16] = 0
    return {"x": x.astype(np.float32).reshape(N, 128, 4 * C).astype(BF), "u": u.reshape(N, 128, 512).astype(BF), "v": v.astype(np.float32).astype(BF), **stored(l), **weights(rng, w.astype(BF))}
def setup_inputs_spread(rng):
    d = setup_inputs(rng)
    d["x"] = wide(rng, N, 128, 4 * C, cols=6)
    return d
def check_inputs(d):
    b = []
    for k in ("x", "u", "v"):
        a = np.abs(d[k].astype(np.float32))
        if not (np.isfinite(a).all() and ((a == 0) | (a >= 2.0 ** -30) & (a <= 2.0 ** 30)).all()): b.append("a value of " + k)
    for k in ("la", "lb"):
        if not ((d[k] >= 0) & (d[k] < C)).all(): b.append("an entry of " + k)
    none, least, most = [emit(mx_ref.quantize(np.full((128, 16), k, np.float32).astype(BF)))[1][0, 0] for k in (0.0, 2.0 ** -8, 2.0 ** 8)]
    for r in range(N):
        if ((d["wc"][r] == 0x7F) | (d["wc"][r] == 0xFF)).any(): b.append("wc: a code that is no number")
        s = mx_ref.live(d["ws"][r])
        if ((s != none) & ((s < least) | (s > most))).any(): b.append("ws: a scale out of range")
        if (((d["wc"][r].reshape(16, 8, 512, 4) & 0x7F) != 0) & (s == none)[:, None, :, None]).any(): b.append("wc: a code other than zero under the scale of zeros")
    return b
def look(t, e):
    return np.take_along_axis(t, e, axis=1)
def leaders(p):
    low, at = np.tile(np.arange(C), (8, 1)), p
    for k in range(DOUBLINGS):
        low = np.minimum(low, look(low, at))
        at = look(at, at)
    return look(low, at)
def reference(x, u, v, la, lb, wc, ws):
    qu = [mx_ref.quantize(u[r]) for r in range(N)]
    lay = [pk(wc[r], ws[r]) for r in range(N)]
    l0, l1 = [gentries(la[r]) for r in range(N)], [gentries(lb[r]) for r in range(N)]
    now = [x[r] for r in range(N)]
    for step in STEP:
        own, torn, sent = [], [], []
        for r in range(N):
            q = mx_ref.quantize(now[r])
            s = mx_ref.matmul(qu[r], q)[::16] + np.float32(0.0)
            p = np.where(s < 0, l1[r], l0[r])
            lead = leaders(p)
            e = np.where(lead == np.arange(C), lead, p)
            own.append(decode(q).astype(BF))
            torn.append(e)
            z = own[r]
            for k in range(3):
                z = ((z.astype(np.float32) + gcols(z, e).astype(np.float32)) * np.float32(0.5)).astype(BF)
                e = look(e, e)
            sent.append(mx_ref.quantize(z))
            change = look(s, lead) > s
            l0[r], l1[r] = np.where(change, l1[r], l0[r]), np.where(change, l0[r], l1[r])
        for r in range(N):
            z = sent[(r - step) % N]
            h = tile([mx_ref.matmul(pick(lay[r], np.arange(128 * b, 128 * b + 128)), z) * np.float32(0.03125) for b in range(4)])
            now[r] = (own[r].astype(np.float32) + gcols(h, torn[r]).astype(np.float32)).astype(BF)
    y, ls = np.zeros((N, 128, C), np.float32), np.zeros((N, 8, 2 * C), np.float32)
    oc, osc = np.zeros((N, 128, 4 * C), np.uint8), np.zeros((N, 16, C), np.uint8)
    for r in range(N):
        q = mx_ref.quantize(now[r])
        y[r] = mx_ref.matmul(mx_ref.quantize(v[r]), q)
        ls[r] = np.concatenate([l0[r], l1[r]], axis=1)
        oc[r], osc[r] = emit(q)
    return {"y": y, "ls": ls, "oc": oc, "osc": osc}

@@ -1,0 +1,257 @@
+from concourse.mybir import dt, AluOpType, ActivationFunctionType
+
+C = 320
+STEP = [1, 2, 4]
+BF, F32, I32, U16 = "bfloat16", "float32", "int32", "uint16"
+
+SCRATCH = {}
+
+
+def _sb(dtype, **kw):
+    for k, n in kw.items():
+        SCRATCH[k] = ("sbuf", [128, n], dtype)
+
+
+_sb(BF, xin=1280, uin=512, vin=512, e8=516, e1=516, iot=320, kk=320, sca=320, mm=320, aw=320 * 8, low=320 * 9,
+    tf=960, bw=960, fw=1280, fo=1280, hw=1280, z1=1280, z2=1280, z3=1280, xt=1280, tmp=640, fl=320, ld=320 * 9, fd=640, d1=1280, d2=1280)
+_sb(F32, iof=320, dj=128, tpos=320, m16=20, kf=1, k1=1, scl=1, cw=20, n0=320, n1=320, sf=320, sg=320, l0w=20, l1w=20, dw=20,
+    mw=20, tp=20, pw=20, dcp=20, ew=20, ed=20, tw=20, lsf=640, yf=320)
+_sb(I32, lai=20, lbi=20, pi=1, ki=1, lwi=20)
+_sb(U16, uo=8, offs=200, l0o=20, l1o=20)
+_sb("float8_e4m3fn_x4", wq=512, qu=128, qup=128, qv=128, qe8=512, qe1=512, qz=320)
+_sb("uint8", wsq=512, su=128, sup=128, sv=128, se8=512, se1=512, sz=320)
+for _i in range(4):
+    SCRATCH["q%d" % _i] = ("sbuf", [128, C], "float8_e4m3fn_x4")
+    SCRATCH["s%d" % _i] = ("sbuf", [128, C], "uint8")
+for _i in range(3):
+    SCRATCH["lq%d" % _i] = ("sbuf", [128, C], "float8_e4m3fn_x4")
+    SCRATCH["lp%d" % _i] = ("sbuf", [128, C], "uint8")
+    SCRATCH["lt%d" % _i] = ("sbuf", [128, 20], U16)
+    SCRATCH["lu%d" % _i] = ("sbuf", [128, 40], U16)
+    SCRATCH["to%d" % _i] = ("sbuf", [128, 20], U16)
+    SCRATCH["tb%d" % _i] = ("sbuf", [128, 40], U16)
+SCRATCH["psa"] = ("psum", [128, 2048], F32)
+SCRATCH["psf"] = ("psum", [128, 1536], F32)
+SCRATCH["pss"] = ("psum", [128, 512], F32)
+
+SEMAPHORES = ["cv", "cs", "ct", "cg", "left", "ldx", "ldu", "ldv", "ldl", "ldw", "sto", "stc"]
+SEMAPHORES += ["%s%d" % (k, i) for k in ("aq", "at", "ab") for i in range(3)]
+
+
+def rank_program(g, core, T, topo):
+    rank = T.rank_of(core)
+    if rank is None:
+        return
+    N = len(T.cores)
+    A = AluOpType
+    COPY = ActivationFunctionType.Copy
+    eng = {"v": g.vector, "s": g.scalar, "t": g.tensor, "g": g, "y": g.sync}
+    cnt = {"v": 0, "s": 0, "t": 0, "g": 0}
+    seen = {}
+
+    def need(q, *toks):
+        most = {}
+        for name, n in toks:
+            most[name] = max(n, most.get(name, 0))
+        for name, n in most.items():
+            if seen.get((q, name), 0) < n:
+                eng[q].wait_ge(T.sem[name], n)
+                seen[(q, name)] = n
+
+    def run(q, deps, fn, *a, **kw):
+        need(q, *deps)
+        ins = fn(*a, **kw)
+        cnt[q] += 1
+        ins.then_inc(T.sem["c" + q], 1)
+        return ("c" + q, cnt[q])
+
+    V, S, TE = g.vector, g.scalar, g.tensor
+
+    def w20(buf):
+        return buf[:, 15:C:16]
+
+    def blk(buf, b, w=C):
+        return buf[:, w * b:w * b + C]
+
+    g.sync.dma_start(T.xin[:], T.x[:, :]).then_inc(T.sem.ldx, 16)
+    g.scalar.dma_start(T.uin[:], T.u[:, :]).then_inc(T.sem.ldu, 16)
+    g.scalar.dma_start(T.lai[:], T.la[:, :]).then_inc(T.sem.ldl, 16)
+    g.scalar.dma_start(T.lbi[:], T.lb[:, :]).then_inc(T.sem.ldl, 16)
+    g.sync.dma_start(T.wq[:, 0:512].bitcast(dt.uint8), T.wc[:, :]).then_inc(T.sem.ldw, 16)
+    g.sync.dma_start(T.wsq[:, 0:512], T.ws[:, :]).then_inc(T.sem.ldw, 16)
+    g.sync.dma_start(T.vin[:], T.v[:, :]).then_inc(T.sem.ldv, 16)
+
+    SMALL = {"allow_small_or_imprecise_dtypes": True}
+    k_m16 = run("g", [], g.iota, T.m16[:], [[16, 20]], 0, 0, **SMALL)
+    k_pi = run("g", [], g.iota, T.pi[:], [[0, 1]], 0, 1)
+    k_dj = run("g", [], g.iota, T.dj[:], [[1, 128]], 0, -1, **SMALL)
+    k_tp = run("g", [], g.iota, T.tpos[:], [[0, 20], [1, 16]], 0, 0, **SMALL)
+    k_io = run("g", [], g.iota, T.iot[:], [[1, C]], -160, 0, **SMALL)
+
+    m8 = run("v", [], V.memset, T.e8[:], 0.0)
+    m1 = run("v", [], V.memset, T.e1[:], 0.0)
+    uo = run("v", [k_m16], V.tensor_copy, T.uo[:], T.m16[:, 0:8])
+    ki = run("v", [k_pi], V.tensor_scalar, T.ki[:], T.pi[:], 15, None, A.bitwise_and)
+    kf = run("v", [ki], V.tensor_copy, T.kf[:], T.ki[:])
+    k1 = run("v", [kf], V.tensor_scalar, T.k1[:], T.kf[:], 1.0, None, A.add)
+    sc = run("v", [kf], V.tensor_scalar, T.scl[:], T.kf[:], 15.0, 1.0 - 2.0 ** -15, A.is_equal, A.mult)
+    sc = run("v", [sc], V.tensor_scalar, T.scl[:], T.scl[:], 2.0 ** -15, None, A.add)
+    cw = run("v", [k_m16, kf], V.tensor_scalar, T.cw[:], T.m16[:], T.kf[:, 0:1], None, A.add)
+    d8 = run("v", [k_dj, m8], V.tensor_scalar, T.e8[:, 3:515:4], T.dj[:], 0.0, 0.125, A.is_equal, A.mult)
+    n0 = run("v", [k_tp, kf], V.tensor_scalar, T.n0[:], T.tpos[:], T.kf[:, 0:1], None, A.not_equal)
+    n1 = run("v", [k_tp, k1], V.tensor_scalar, T.n1[:], T.tpos[:], T.k1[:, 0:1], 32767.0, A.is_equal, A.mult)
+    kk = run("v", [n0, n1], V.tensor_tensor, T.kk[:], T.n0[:], T.n1[:], A.add)
+    qe8 = None
+    for b in range(4):
+        qe8 = run("v", [d8], V.quantize_mx, T.qe8[:, 128 * b:128 * b + 128], T.se8[:, 128 * b:128 * b + 128], T.e8[:, 3 - b:515 - b])
+
+    a = run("v", [("ldu", 16)], V.quantize_mx, T.qu[:, 0:128], T.su[:, 0:128], T.uin[:])
+    run("v", [a, uo], V.tensor_copy, T.qup[:, 0:128].bitcast(dt.uint32), T.qu[:, 0:128].bitcast(dt.uint32).indirect(T.uo[:, 0:8]))
+    qup = run("v", [a, uo], V.tensor_copy, T.sup[:, 0:128], T.su[:, 0:128].indirect(T.uo[:, 0:8]))
+    tq = run("v", [("ldx", 16)], V.quantize_mx, T.q0[:, 0:C], T.s0[:, 0:C], T.xin[:])
+    l0 = run("v", [("ldl", 32)], V.tensor_copy, T.l0w[:], T.lai[:])
+    l1 = run("v", [("ldl", 32)], V.tensor_copy, T.l1w[:], T.lbi[:])
+    dw = run("v", [l0, l1], V.tensor_tensor, T.dw[:], T.l1w[:], T.l0w[:], A.subtract)
+
+    def conv(src, dep, out, bias, war=()):
+        a = run("v", [dep, kk, ("cv", cnt["v"])], V.tensor_tensor_scan, T.sca[:], T.kk[:], src, 0.0, A.mult, A.add)
+        return run("v", [a, sc] + list(war), V.tensor_scalar, out, w20(T.sca), T.scl[:, 0:1], bias, A.mult, A.add)
+
+    left = 0
+    f3 = ("cs", 0)
+    tx = None
+    qe1 = None
+    for i, d in enumerate(STEP):
+        q, s = T["q%d" % i], T["s%d" % i]
+        lq, lp, lt, lu, to, tb = T["lq%d" % i], T["lp%d" % i], T["lt%d" % i], T["lu%d" % i], T["to%d" % i], T["tb%d" % i]
+        dst = T.cores[(rank + d) % N]
+        src = T.cores[(rank - d) % N]
+        rid, pid, _ = topo.addr(dst)
+        mask = topo.mask(core, dst)
+        ne, na = len(topo.engines(core, dst)), len(topo.engines(src, core))
+
+        def send(out, in_, sem):
+            g.remote_dma(out, in_, T.sem[sem], T.sem.left, pid, rid, mask)
+
+        need("g", tq)
+        send(lq[:, 0:C].bitcast(dt.uint8), q[:, 0:C].bitcast(dt.uint8), "aq%d" % i)
+        send(lp[:, 0:C], s[:, 0:C], "aq%d" % i)
+        if i == 0:
+            k_if = run("g", [], g.iota, T.iof[:], [[1, C]], 0, 0, **SMALL)
+
+        ts = run("t", [tq, qup, f3], TE.matmul_mx, T.pss[:, 0:C], T.qup[:, 0:128], T.sup[:, 0:128], q[:, 0:C], s[:, 0:C], True, True)
+        m = run("v", [ts, ("cv", cnt["v"])], V.tensor_scalar, T.mm[:], T.pss[:, 0:C], 0.0, None, A.is_lt)
+        sfull = run("s", [m], S.activation, T.sf[:], T.pss[:, 0:C], COPY)
+        a = run("v", [m, kk], V.tensor_tensor_scan, T.sca[:], T.kk[:], T.mm[:], 0.0, A.mult, A.add)
+        a = run("v", [a, sc], V.tensor_scalar, T.mw[:], w20(T.sca), T.scl[:, 0:1], 0.5, A.mult, A.is_gt)
+        a = run("v", [a, dw], V.tensor_tensor, T.tp[:], T.mw[:], T.dw[:], A.mult)
+        pw = run("v", [a], V.tensor_tensor, T.pw[:], T.tp[:], T.l0w[:], A.add)
+
+        def off(k):
+            return T.offs[:, 20 * k:20 * k + 20]
+        o = run("v", [pw], V.tensor_copy, off(0), T.pw[:])
+        dcp = run("v", [pw, cw], V.tensor_tensor, T.dcp[:], T.cw[:], T.pw[:], A.subtract)
+
+        ak = run("s", [o, k_io], S.activation, blk(T.aw, 0), T.iot[:, 0:C].indirect(off(0)), COPY)
+        low, lowt = blk(T.aw, 0), ak
+        dup = run("v", [ak], V.tensor_copy, blk(T.ld, 0), low)
+        for k in range(7):
+            an = run("s", [ak, o], S.activation, blk(T.aw, k + 1), blk(T.aw, k).indirect(off(k)), COPY)
+            lowt = run("v", [lowt, o, ak, dup], V.tensor_tensor, blk(T.low, k), low.indirect(off(k)), blk(T.ld, k), A.min)
+            low = blk(T.low, k)
+            dup = run("s", [lowt], S.activation, blk(T.ld, k + 1), low, COPY)
+            o = conv(blk(T.aw, k + 1), an, off(k + 1), 160.25)
+            ak = an
+        lowt = run("v", [lowt, o, dup], V.tensor_tensor, blk(T.low, 7), low.indirect(off(7)), blk(T.ld, 7), A.min)
+        low = blk(T.low, 7)
+        dup = run("v", [lowt], V.tensor_copy, blk(T.ld, 8), low)
+        lowt = run("v", [lowt, dup], V.tensor_tensor, blk(T.low, 8), low.indirect(off(6)), blk(T.ld, 8), A.min)
+        low = blk(T.low, 8)
+        a = conv(low, lowt, T.lwi[:], 160.25)
+        a = run("v", [a, cw], V.tensor_tensor, T.ew[:], T.lwi[:], T.cw[:], A.is_equal)
+        a = run("v", [a, dcp], V.tensor_tensor, T.ed[:], T.ew[:], T.dcp[:], A.mult)
+        a = run("v", [a], V.tensor_tensor, T.tw[:], T.ed[:], T.pw[:], A.add)
+        tt = run("v", [a], V.tensor_copy, to[:, 0:20], T.tw[:])
+        need("g", tt)
+        send(lt[:, 0:20], to[:, 0:20], "at%d" % i)
+
+        arr = ("aq%d" % i, 2 * na)
+        f8 = [run("t", [arr, qe8, sfull], TE.matmul_mx, T.psa[:, 512 * b:512 * b + C], T.qe8[:, 128 * b:128 * b + 128],
+                  T.se8[:, 128 * b:128 * b + 128], lq[:, 0:C], lp[:, 0:C], True, True) for b in range(4)]
+        fw = [run("s", [f8[b]], S.activation, blk(T.fw, b), T.psa[:, 512 * b:512 * b + C], COPY) for b in range(4)]
+
+        fd = [run("v", [fw[b]], V.tensor_copy, blk(T.fd, b), blk(T.fw, b)) for b in (0, 1)]
+
+        t1 = run("s", [tt], S.activation, blk(T.tf, 0), T.iot[:, 0:C].indirect(to[:, 0:20]), COPY)
+        t2 = run("s", [t1], S.activation, blk(T.tf, 1), blk(T.tf, 0).indirect(to[:, 0:20]), COPY)
+        b1 = run("s", [lowt], S.activation, blk(T.bw, 0), low.indirect(off(7)), COPY)
+        o2 = conv(blk(T.tf, 1), t2, tb[:, 0:20], 160.25)
+        t4 = run("s", [o2], S.activation, blk(T.tf, 2), blk(T.tf, 1).indirect(tb[:, 0:20]), COPY)
+        b2 = run("s", [b1], S.activation, blk(T.bw, 1), blk(T.bw, 0).indirect(off(7)), COPY)
+        b3 = run("s", [b2], S.activation, blk(T.bw, 2), blk(T.bw, 1).indirect(off(6)), COPY)
+        sg = run("s", [sfull], S.activation, T.sg[:], T.sf[:], COPY)
+        o4 = conv(blk(T.tf, 2), t4, tb[:, 20:40], 160.25)
+        need("g", o4)
+        send(lu[:, 0:40], tb[:, 0:40], "ab%d" % i)
+        left += 4 * ne
+        if i == 0:
+            d1 = run("v", [k_dj, m1], V.tensor_scalar, T.e1[:, 3:515:4], T.dj[:], 0.0, 1.0, A.is_equal, A.mult)
+            for b in range(4):
+                qe1 = run("v", [d1], V.quantize_mx, T.qe1[:, 128 * b:128 * b + 128], T.se1[:, 128 * b:128 * b + 128], T.e1[:, 3 - b:515 - b])
+        ro = conv(blk(T.bw, 2), b3, off(8), 160.25)
+
+        fbank = [T.psf[:, 0:C], T.psf[:, 512:512 + C], T.psf[:, 1024:1024 + C], T.pss[:, 0:C]]
+        ff = [run("t", [qe1, sfull], TE.matmul_mx, fbank[b], T.qe1[:, 128 * b:128 * b + 128], T.se1[:, 128 * b:128 * b + 128],
+                  q[:, 0:C], s[:, 0:C], True, True) for b in range(4)]
+
+        at, ab = ("at%d" % i, na), ("ab%d" % i, na)
+        zs = [run("s", [at, fw[b]], S.activation, blk(T.tmp, b - 2), blk(T.fw, b).indirect(lt[:, 0:20]), COPY) for b in (2, 3)]
+        z1 = [run("v", [at, fw[b], fd[b]], V.tensor_tensor, blk(T.z1, b), blk(T.fw, b).indirect(lt[:, 0:20]), blk(T.fd, b), A.add) for b in (0, 1)]
+        z1 += [run("v", [zs[b - 2]], V.tensor_tensor, blk(T.z1, b), blk(T.tmp, b - 2), T.psa[:, 512 * b:512 * b + C], A.add) for b in (2, 3)]
+        d1 = [run("s", [z1[b]], S.activation, blk(T.d1, b), blk(T.z1, b), COPY) for b in range(4)]
+        z2 = [run("v", [ab, z1[b], d1[b]], V.tensor_tensor, blk(T.z2, b), blk(T.z1, b).indirect(lu[:, 0:20]), blk(T.d1, b), A.add) for b in range(4)]
+        d2 = [run("s", [z2[b]], S.activation, blk(T.d2, b), blk(T.z2, b), COPY) for b in range(4)]
+        z3 = [run("v", [z2[b], d2[b]], V.tensor_tensor, T.z3[:, b:1280:4], blk(T.z2, b).indirect(lu[:, 20:40]), blk(T.d2, b), A.add) for b in range(4)]
+        tz = run("v", z3, V.quantize_mx, T.qz[:, 0:C], T.sz[:, 0:C], T.z3[:])
+        fo = [run("s", [ff[b]], S.activation, blk(T.fo, b), fbank[b], COPY) for b in range(4)]
+        f3 = fo[3]
+
+        hh = [run("t", [tz, ("ldw", 32), fw[3]], TE.matmul_mx, T.psa[:, 512 * b:512 * b + C], T.wq[:, 128 * b:128 * b + 128],
+                  T.wsq[:, 128 * b:128 * b + 128], T.qz[:, 0:C], T.sz[:, 0:C], True, True) for b in range(4)]
+        hw = [run("s", [hh[b]], S.activation, blk(T.hw, b), T.psa[:, 512 * b:512 * b + C], COPY, scale=0.03125) for b in range(4)]
+
+        a = run("v", [ro, sg], V.tensor_tensor, T.fl[:], T.sf[:, 0:C].indirect(off(8)), T.sg[:, 0:C], A.is_gt)
+        a = run("v", [a], V.tensor_tensor_scan, T.sca[:], T.kk[:], T.fl[:], 0.0, A.mult, A.add)
+        a = run("v", [a], V.tensor_scalar, T.ew[:], w20(T.sca), T.scl[:, 0:1], 0.5, A.mult, A.is_gt)
+        a = run("v", [a], V.tensor_tensor, T.ed[:], T.ew[:], T.dw[:], A.mult)
+        l0 = run("v", [a], V.tensor_tensor, T.l0w[:], T.l0w[:], T.ed[:], A.add)
+        l1 = run("v", [a], V.tensor_tensor, T.l1w[:], T.l1w[:], T.ed[:], A.subtract)
+        if i < 2:
+            dw = run("v", [l0, l1], V.tensor_tensor, T.dw[:], T.l1w[:], T.l0w[:], A.subtract)
+        else:
+            a = run("v", [l0], V.tensor_copy, T.l0o[:], T.l0w[:])
+            b = run("v", [l1], V.tensor_copy, T.l1o[:], T.l1w[:])
+            a = run("s", [a, k_if], S.activation, T.lsf[:, 0:C], T.iof[:, 0:C].indirect(T.l0o[:, 0:20]), COPY)
+            lsd = run("s", [b, k_if], S.activation, T.lsf[:, C:2 * C], T.iof[:, 0:C].indirect(T.l1o[:, 0:20]), COPY)
+
+        tx = [run("v", [hw[b], fo[b], tt], V.tensor_tensor, T.xt[:, b:1280:4], blk(T.hw, b).indirect(to[:, 0:20]), blk(T.fo, b), A.add) for b in range(4)]
+        tq = run("v", tx, V.quantize_mx, T["q%d" % (i + 1)][:, 0:C], T["s%d" % (i + 1)][:, 0:C], T.xt[:])
+        if i == 0:
+            qv = run("v", [("ldv", 16)], V.quantize_mx, T.qv[:, 0:128], T.sv[:, 0:128], T.vin[:])
+
+    need("y", lsd)
+    g.sync.dma_start(T.ls[:, :], T.lsf[0:128:16, :]).then_inc(T.sem.sto, 16)
+    yy = [run("t", [tq, qv, hw[3]], TE.matmul_mx, T.psa[:, 512 * h:512 * h + 160], T.qv[:, 0:128], T.sv[:, 0:128],
+              T.q3[:, 160 * h:160 * h + 160], T.s3[:, 160 * h:160 * h + 160], True, True) for h in (0, 1)]
+    need("y", tq)
+    g.sync.dma_start(T.oc[:, :], T.q3[:, 0:C].bitcast(dt.uint8)).then_inc(T.sem.sto, 16)
+    ya = run("v", [yy[0]], V.tensor_copy, T.yf[:, 0:160], T.psa[:, 0:160])
+    yb = run("s", [yy[1]], S.activation, T.yf[:, 160:320], T.psa[:, 512:672], COPY)
+    need("y", ya)
+    g.sync.dma_start(T.y[:, 0:160], T.yf[:, 0:160]).then_inc(T.sem.sto, 16)
+    need("s", yb, tq)
+    g.scalar.dma_start(T.y[:, 160:320], T.yf[:, 160:320]).then_inc(T.sem.stc, 16)
+    for k in range(4):
+        e, sem = (g.sync, T.sem.sto) if k < 2 else (g.scalar, T.sem.stc)
+        e.dma_start(T.osc[4 * k:4 * k + 4, :], T.s3[32 * k:32 * k + 4, 0:C]).then_inc(sem, 16)
+    need("g", ("cv", cnt["v"]), ("cs", cnt["s"]), ("ct", cnt["t"]), ("cg", cnt["g"]), ("left", left), ("sto", 80), ("stc", 48))

@@ -1,6 +1,7 @@
 from concourse.mybir import dt, AluOpType, ActivationFunctionType
 
 C = 320
+H = 160
 STEP = [1, 2, 4]
 BF, F32, I32, U16 = "bfloat16", "float32", "int32", "uint16"
 
@@ -12,12 +13,13 @@ def _sb(dtype, **kw):
         SCRATCH[k] = ("sbuf", [128, n], dtype)
 
 
-_sb(BF, xin=1280, uin=512, vin=512, e8=516, e1=516, iot=320, kk=320, sca=320, mm=320, aw=320 * 8, low=320 * 9,
-    tf=960, bw=960, fw=1280, fo=1280, hw=1280, z1=1280, z2=1280, z3=1280, xt=1280, tmp=640, fl=320, ld=320 * 9, fd=640, d1=1280, d2=1280)
-_sb(F32, iof=320, dj=128, tpos=320, m16=20, kf=1, k1=1, scl=1, cw=20, n0=320, n1=320, sf=320, sg=320, l0w=20, l1w=20, dw=20,
-    mw=20, tp=20, pw=20, dcp=20, ew=20, ed=20, tw=20, lsf=640, yf=320)
+_sb(BF, xin=1280, uin=512, vin=512, e8=516, e1=516, iot=320, tpos=320, n0=320, n1=320, kk=320, sca=320, mm=320,
+    aw=320 * 8, low=320 * 9, tf=960, bw=960, fw=1280, fo=1280, hw=1280, z1=1280, z2=1280, z3=1280, xt=1280, tmp=640,
+    fl=320, ld=320 * 9, fd=640, d1=1280, d2=1280)
+_sb(F32, iof=320, dj=128, m16=20, kf=1, k1=1, scl=1, scm=1, thr=1, inv=1, cw=20, cb=20, sf=320, sg=320, l0w=20, l1w=20,
+    dw=20, tp=20, pw=20, dcp=20, ew=20, ed=20, eg=20, tw=20, lsf=640, yf=320)
 _sb(I32, lai=20, lbi=20, pi=1, ki=1, lwi=20)
-_sb(U16, uo=8, offs=200, l0o=20, l1o=20)
+_sb(U16, uo=8, offs=180, l0o=20, l1o=20)
 _sb("float8_e4m3fn_x4", wq=512, qu=128, qup=128, qv=128, qe8=512, qe1=512, qz=320)
 _sb("uint8", wsq=512, su=128, sup=128, sv=128, se8=512, se1=512, sz=320)
 for _i in range(4):
@@ -26,16 +28,14 @@ for _i in range(4):
 for _i in range(3):
     SCRATCH["lq%d" % _i] = ("sbuf", [128, C], "float8_e4m3fn_x4")
     SCRATCH["lp%d" % _i] = ("sbuf", [128, C], "uint8")
-    SCRATCH["lt%d" % _i] = ("sbuf", [128, 20], U16)
-    SCRATCH["lu%d" % _i] = ("sbuf", [128, 40], U16)
-    SCRATCH["to%d" % _i] = ("sbuf", [128, 20], U16)
-    SCRATCH["tb%d" % _i] = ("sbuf", [128, 40], U16)
+    for _k in ("ta", "tb", "tc", "la_", "lb_", "lc_"):
+        SCRATCH["%s%d" % (_k, _i)] = ("sbuf", [128, 20], U16)
 SCRATCH["psa"] = ("psum", [128, 2048], F32)
 SCRATCH["psf"] = ("psum", [128, 1536], F32)
 SCRATCH["pss"] = ("psum", [128, 512], F32)
 
-SEMAPHORES = ["cv", "cs", "ct", "cg", "left", "ldx", "ldu", "ldv", "ldl", "ldw", "sto", "stc"]
-SEMAPHORES += ["%s%d" % (k, i) for k in ("aq", "at", "ab") for i in range(3)]
+SEMAPHORES = ["cv", "cs", "ct", "cg", "left", "ldx", "ldy", "ldu", "ldv", "ldl", "ldw", "sto", "stc"]
+SEMAPHORES += ["%s%d" % (k, i) for k in ("aq", "at", "ab", "ac") for i in range(3)]
 
 
 def rank_program(g, core, T, topo):
@@ -70,13 +70,18 @@ def rank_program(g, core, T, topo):
     def w20(buf):
         return buf[:, 15:C:16]
 
-    def blk(buf, b, w=C):
-        return buf[:, w * b:w * b + C]
+    def blk(buf, b):
+        return buf[:, C * b:C * b + C]
 
-    g.sync.dma_start(T.xin[:], T.x[:, :]).then_inc(T.sem.ldx, 16)
+    def mov(buf, b):
+        return buf[:, 128 * b:128 * b + 128]
+
+    g.sync.dma_start(T.xin[:, 0:640], T.x[:, 0:640]).then_inc(T.sem.ldx, 16)
     g.scalar.dma_start(T.uin[:], T.u[:, :]).then_inc(T.sem.ldu, 16)
-    g.scalar.dma_start(T.lai[:], T.la[:, :]).then_inc(T.sem.ldl, 16)
-    g.scalar.dma_start(T.lbi[:], T.lb[:, :]).then_inc(T.sem.ldl, 16)
+    g.scalar.dma_start(T.xin[:, 640:1280], T.x[:, 640:1280]).then_inc(T.sem.ldy, 16)
+    g.sync.dma_start(T.lai[:], T.la[:, :]).then_inc(T.sem.ldl, 16)
+    g.sync.dma_start(T.lbi[:], T.lb[:, :]).then_inc(T.sem.ldl, 16)
+    need("y", ("ldx", 16), ("ldy", 16))
     g.sync.dma_start(T.wq[:, 0:512].bitcast(dt.uint8), T.wc[:, :]).then_inc(T.sem.ldw, 16)
     g.sync.dma_start(T.wsq[:, 0:512], T.ws[:, :]).then_inc(T.sem.ldw, 16)
     g.sync.dma_start(T.vin[:], T.v[:, :]).then_inc(T.sem.ldv, 16)
@@ -84,8 +89,8 @@ def rank_program(g, core, T, topo):
     SMALL = {"allow_small_or_imprecise_dtypes": True}
     k_m16 = run("g", [], g.iota, T.m16[:], [[16, 20]], 0, 0, **SMALL)
     k_pi = run("g", [], g.iota, T.pi[:], [[0, 1]], 0, 1)
-    k_dj = run("g", [], g.iota, T.dj[:], [[1, 128]], 0, -1, **SMALL)
     k_tp = run("g", [], g.iota, T.tpos[:], [[0, 20], [1, 16]], 0, 0, **SMALL)
+    k_dj = run("g", [], g.iota, T.dj[:], [[1, 128]], 0, -1, **SMALL)
     k_io = run("g", [], g.iota, T.iot[:], [[1, C]], -160, 0, **SMALL)
 
     m8 = run("v", [], V.memset, T.e8[:], 0.0)
@@ -94,63 +99,89 @@ def rank_program(g, core, T, topo):
     ki = run("v", [k_pi], V.tensor_scalar, T.ki[:], T.pi[:], 15, None, A.bitwise_and)
     kf = run("v", [ki], V.tensor_copy, T.kf[:], T.ki[:])
     k1 = run("v", [kf], V.tensor_scalar, T.k1[:], T.kf[:], 1.0, None, A.add)
-    sc = run("v", [kf], V.tensor_scalar, T.scl[:], T.kf[:], 15.0, 1.0 - 2.0 ** -15, A.is_equal, A.mult)
-    sc = run("v", [sc], V.tensor_scalar, T.scl[:], T.scl[:], 2.0 ** -15, None, A.add)
-    cw = run("v", [k_m16, kf], V.tensor_scalar, T.cw[:], T.m16[:], T.kf[:, 0:1], None, A.add)
-    d8 = run("v", [k_dj, m8], V.tensor_scalar, T.e8[:, 3:515:4], T.dj[:], 0.0, 0.125, A.is_equal, A.mult)
+    a = run("v", [kf], V.tensor_scalar, T.scl[:], T.kf[:], 15.0, 1.0 - 2.0 ** -15, A.is_equal, A.mult)
+    b = run("v", [kf], V.tensor_scalar, T.inv[:], T.kf[:], 15.0, 1.0 - 2.0 ** 15, A.is_equal, A.mult)
+    sc = run("v", [a], V.tensor_scalar, T.scl[:], T.scl[:], 2.0 ** -15, None, A.add)
+    b = run("v", [b], V.tensor_scalar, T.inv[:], T.inv[:], 2.0 ** 15, None, A.add)
     n0 = run("v", [k_tp, kf], V.tensor_scalar, T.n0[:], T.tpos[:], T.kf[:, 0:1], None, A.not_equal)
-    n1 = run("v", [k_tp, k1], V.tensor_scalar, T.n1[:], T.tpos[:], T.k1[:, 0:1], 32767.0, A.is_equal, A.mult)
-    kk = run("v", [n0, n1], V.tensor_tensor, T.kk[:], T.n0[:], T.n1[:], A.add)
-    qe8 = None
-    for b in range(4):
-        qe8 = run("v", [d8], V.quantize_mx, T.qe8[:, 128 * b:128 * b + 128], T.se8[:, 128 * b:128 * b + 128], T.e8[:, 3 - b:515 - b])
+    n1 = run("v", [k_tp, k1], V.tensor_scalar, T.n1[:], T.tpos[:], T.k1[:, 0:1], 2.0 ** 15, A.is_equal, A.mult)
+    cw = run("v", [k_m16, kf], V.tensor_scalar, T.cw[:], T.m16[:], T.kf[:, 0:1], None, A.add)
+    cb = run("v", [k_m16, kf], V.tensor_scalar, T.cb[:], T.m16[:], T.kf[:, 0:1], 0.25, A.add, A.add)
+    kk = run("v", [n0, n1], V.tensor_tensor, T.kk[:], T.n0[:], T.n1[:], A.max)
+    d8 = run("v", [k_dj, m8], V.tensor_scalar, T.e8[:, 3:515:4], T.dj[:], 0.0, 0.125, A.is_equal, A.mult)
+    run("v", [sc], V.tensor_scalar, T.scm[:], T.scl[:], -2.0, None, A.mult)
+    run("v", [b], V.tensor_scalar, T.thr[:], T.inv[:], 0.5, None, A.mult)
+
+    def diagonal(e, q, s, dep):
+        return [run("v", [dep], V.quantize_mx, mov(q, b), mov(s, b), e[:, 3 - b:515 - b]) for b in range(4)][3]
+
+    qe8 = diagonal(T.e8, T.qe8, T.se8, d8)
 
     a = run("v", [("ldu", 16)], V.quantize_mx, T.qu[:, 0:128], T.su[:, 0:128], T.uin[:])
     run("v", [a, uo], V.tensor_copy, T.qup[:, 0:128].bitcast(dt.uint32), T.qu[:, 0:128].bitcast(dt.uint32).indirect(T.uo[:, 0:8]))
     qup = run("v", [a, uo], V.tensor_copy, T.sup[:, 0:128], T.su[:, 0:128].indirect(T.uo[:, 0:8]))
-    tq = run("v", [("ldx", 16)], V.quantize_mx, T.q0[:, 0:C], T.s0[:, 0:C], T.xin[:])
-    l0 = run("v", [("ldl", 32)], V.tensor_copy, T.l0w[:], T.lai[:])
-    l1 = run("v", [("ldl", 32)], V.tensor_copy, T.l1w[:], T.lbi[:])
-    dw = run("v", [l0, l1], V.tensor_tensor, T.dw[:], T.l1w[:], T.l0w[:], A.subtract)
 
-    def conv(src, dep, out, bias, war=()):
-        a = run("v", [dep, kk, ("cv", cnt["v"])], V.tensor_tensor_scan, T.sca[:], T.kk[:], src, 0.0, A.mult, A.add)
-        return run("v", [a, sc] + list(war), V.tensor_scalar, out, w20(T.sca), T.scl[:, 0:1], bias, A.mult, A.add)
+    def quant(tile, i, deps):
+        return [run("v", deps[h], V.quantize_mx, T["q%d" % i][:, H * h:H * h + H], T["s%d" % i][:, H * h:H * h + H],
+                    tile[:, 4 * H * h:4 * H * h + 4 * H]) for h in (0, 1)]
+
+    tq = quant(T.xin, 0, [[("ldx", 16)], [("ldy", 16)]])
+    l0 = run("v", [("ldl", 32)], V.tensor_scalar, T.l0w[:], T.lai[:], 0.25, None, A.add)
+    l1 = run("v", [("ldl", 32)], V.tensor_scalar, T.l1w[:], T.lbi[:], 0.25, None, A.add)
+    a = run("v", [l0, l1], V.tensor_tensor, T.dw[:], T.l1w[:], T.l0w[:], A.subtract)
+    dw = run("v", [a, sc], V.tensor_scalar, T.dw[:], T.dw[:], T.scl[:, 0:1], None, A.mult)
+
+    def scan(src, deps):
+        return run("v", list(deps) + [kk, ("cv", cnt["v"])], V.tensor_tensor_scan, T.sca[:], T.kk[:], src, 0.0, A.mult, A.add)
+
+    def conv(src, dep, out):
+        a = scan(src, [dep])
+        return run("v", [a, sc], V.tensor_scalar, out, w20(T.sca), T.scl[:, 0:1], 160.25, A.mult, A.add)
+
+    def off(k):
+        return T.offs[:, 20 * k:20 * k + 20]
 
     left = 0
-    f3 = ("cs", 0)
-    tx = None
     qe1 = None
     for i, d in enumerate(STEP):
         q, s = T["q%d" % i], T["s%d" % i]
-        lq, lp, lt, lu, to, tb = T["lq%d" % i], T["lp%d" % i], T["lt%d" % i], T["lu%d" % i], T["to%d" % i], T["tb%d" % i]
+        lq, lp = T["lq%d" % i], T["lp%d" % i]
+        ta, tb, tc = [T["%s%d" % (k, i)] for k in ("ta", "tb", "tc")]
+        la, lb, lc = [T["%s%d" % (k, i)] for k in ("la_", "lb_", "lc_")]
         dst = T.cores[(rank + d) % N]
         src = T.cores[(rank - d) % N]
         rid, pid, _ = topo.addr(dst)
         mask = topo.mask(core, dst)
         ne, na = len(topo.engines(core, dst)), len(topo.engines(src, core))
 
-        def send(out, in_, sem):
-            g.remote_dma(out, in_, T.sem[sem], T.sem.left, pid, rid, mask)
+        def send(out, in_, sem, dep):
+            need("g", dep)
+            g.remote_dma(out, in_, T.sem["%s%d" % (sem, i)], T.sem.left, pid, rid, mask)
 
-        need("g", tq)
-        send(lq[:, 0:C].bitcast(dt.uint8), q[:, 0:C].bitcast(dt.uint8), "aq%d" % i)
-        send(lp[:, 0:C], s[:, 0:C], "aq%d" % i)
+        send(lq[:, 0:C].bitcast(dt.uint8), q[:, 0:C].bitcast(dt.uint8), "aq", tq[1])
+        send(lp[:, 0:C], s[:, 0:C], "aq", tq[1])
         if i == 0:
             k_if = run("g", [], g.iota, T.iof[:], [[1, C]], 0, 0, **SMALL)
 
-        ts = run("t", [tq, qup, f3], TE.matmul_mx, T.pss[:, 0:C], T.qup[:, 0:128], T.sup[:, 0:128], q[:, 0:C], s[:, 0:C], True, True)
-        m = run("v", [ts, ("cv", cnt["v"])], V.tensor_scalar, T.mm[:], T.pss[:, 0:C], 0.0, None, A.is_lt)
-        sfull = run("s", [m], S.activation, T.sf[:], T.pss[:, 0:C], COPY)
-        a = run("v", [m, kk], V.tensor_tensor_scan, T.sca[:], T.kk[:], T.mm[:], 0.0, A.mult, A.add)
-        a = run("v", [a, sc], V.tensor_scalar, T.mw[:], w20(T.sca), T.scl[:, 0:1], 0.5, A.mult, A.is_gt)
-        a = run("v", [a, dw], V.tensor_tensor, T.tp[:], T.mw[:], T.dw[:], A.mult)
-        pw = run("v", [a], V.tensor_tensor, T.pw[:], T.tp[:], T.l0w[:], A.add)
-
-        def off(k):
-            return T.offs[:, 20 * k:20 * k + 20]
+        sbank = [T.pss[:, 0:H], T.psf[:, 0:H]]
+        ts = [run("t", [tq[h], qup], TE.matmul_mx, sbank[h], T.qup[:, 0:128], T.sup[:, 0:128],
+                  q[:, H * h:H * h + H], s[:, H * h:H * h + H], True, True) for h in (0, 1)]
+        m = [run("v", [ts[h]], V.tensor_scalar, T.mm[:, H * h:H * h + H], sbank[h], 0.0, None, A.is_lt) for h in (0, 1)]
+        if i:
+            dw = run("v", [eg], V.tensor_tensor, T.dw[:], T.dw[:], T.eg[:], A.add)
+        a = run("v", m + [kk], V.tensor_tensor_scan, T.sca[:], T.kk[:], T.mm[:], 0.0, A.mult, A.add)
+        a = run("v", [a, dw], V.tensor_tensor, T.tp[:], w20(T.sca), T.dw[:], A.mult)
+        pw = run("v", [a, l0], V.tensor_tensor, T.pw[:], T.tp[:], T.l0w[:], A.add)
         o = run("v", [pw], V.tensor_copy, off(0), T.pw[:])
-        dcp = run("v", [pw, cw], V.tensor_tensor, T.dcp[:], T.cw[:], T.pw[:], A.subtract)
+        sf = [run("s", [m[h]], S.activation, T.sf[:, H * h:H * h + H], sbank[h], COPY) for h in (0, 1)]
+        dcp = run("v", [pw, cb], V.tensor_tensor, T.dcp[:], T.cb[:], T.pw[:], A.subtract)
+        if i == 0:
+            qe1 = diagonal(T.e1, T.qe1, T.se1, run("v", [k_dj, m1], V.tensor_scalar, T.e1[:, 3:515:4], T.dj[:], 0.0, 1.0, A.is_equal, A.mult))
+
+        if i:
+            run("v", [e], V.tensor_tensor, T.l1w[:], T.l1w[:], T.ed[:], A.subtract)
+        if i == 1:
+            qv = run("v", [("ldv", 16)], V.quantize_mx, T.qv[:, 0:128], T.sv[:, 0:128], T.vin[:])
 
         ak = run("s", [o, k_io], S.activation, blk(T.aw, 0), T.iot[:, 0:C].indirect(off(0)), COPY)
         low, lowt = blk(T.aw, 0), ak
@@ -160,98 +191,92 @@ def rank_program(g, core, T, topo):
             lowt = run("v", [lowt, o, ak, dup], V.tensor_tensor, blk(T.low, k), low.indirect(off(k)), blk(T.ld, k), A.min)
             low = blk(T.low, k)
             dup = run("s", [lowt], S.activation, blk(T.ld, k + 1), low, COPY)
-            o = conv(blk(T.aw, k + 1), an, off(k + 1), 160.25)
+            o = conv(blk(T.aw, k + 1), an, off(k + 1))
             ak = an
         lowt = run("v", [lowt, o, dup], V.tensor_tensor, blk(T.low, 7), low.indirect(off(7)), blk(T.ld, 7), A.min)
         low = blk(T.low, 7)
         dup = run("v", [lowt], V.tensor_copy, blk(T.ld, 8), low)
         lowt = run("v", [lowt, dup], V.tensor_tensor, blk(T.low, 8), low.indirect(off(6)), blk(T.ld, 8), A.min)
         low = blk(T.low, 8)
-        a = conv(low, lowt, T.lwi[:], 160.25)
+        a = conv(low, lowt, T.lwi[:])
         a = run("v", [a, cw], V.tensor_tensor, T.ew[:], T.lwi[:], T.cw[:], A.is_equal)
         a = run("v", [a, dcp], V.tensor_tensor, T.ed[:], T.ew[:], T.dcp[:], A.mult)
         a = run("v", [a], V.tensor_tensor, T.tw[:], T.ed[:], T.pw[:], A.add)
-        tt = run("v", [a], V.tensor_copy, to[:, 0:20], T.tw[:])
-        need("g", tt)
-        send(lt[:, 0:20], to[:, 0:20], "at%d" % i)
+        tt = run("v", [a], V.tensor_copy, ta[:, 0:20], T.tw[:])
+        send(la[:, 0:20], ta[:, 0:20], "at", tt)
 
-        arr = ("aq%d" % i, 2 * na)
-        f8 = [run("t", [arr, qe8, sfull], TE.matmul_mx, T.psa[:, 512 * b:512 * b + C], T.qe8[:, 128 * b:128 * b + 128],
-                  T.se8[:, 128 * b:128 * b + 128], lq[:, 0:C], lp[:, 0:C], True, True) for b in range(4)]
+        f8 = [run("t", [("aq%d" % i, 2 * na), qe8, sf[1]], TE.matmul_mx, T.psa[:, 512 * b:512 * b + C], mov(T.qe8, b), mov(T.se8, b),
+                  lq[:, 0:C], lp[:, 0:C], True, True) for b in range(4)]
         fw = [run("s", [f8[b]], S.activation, blk(T.fw, b), T.psa[:, 512 * b:512 * b + C], COPY) for b in range(4)]
-
         fd = [run("v", [fw[b]], V.tensor_copy, blk(T.fd, b), blk(T.fw, b)) for b in (0, 1)]
 
-        t1 = run("s", [tt], S.activation, blk(T.tf, 0), T.iot[:, 0:C].indirect(to[:, 0:20]), COPY)
-        t2 = run("s", [t1], S.activation, blk(T.tf, 1), blk(T.tf, 0).indirect(to[:, 0:20]), COPY)
-        b1 = run("s", [lowt], S.activation, blk(T.bw, 0), low.indirect(off(7)), COPY)
-        o2 = conv(blk(T.tf, 1), t2, tb[:, 0:20], 160.25)
-        t4 = run("s", [o2], S.activation, blk(T.tf, 2), blk(T.tf, 1).indirect(tb[:, 0:20]), COPY)
-        b2 = run("s", [b1], S.activation, blk(T.bw, 1), blk(T.bw, 0).indirect(off(7)), COPY)
+        t1 = run("s", [tt], S.activation, blk(T.tf, 0), T.iot[:, 0:C].indirect(ta[:, 0:20]), COPY)
+        t2 = run("s", [t1], S.activation, blk(T.tf, 1), blk(T.tf, 0).indirect(ta[:, 0:20]), COPY)
+        sg = run("s", [sf[1]], S.activation, T.sg[:], T.sf[:], COPY)
+        b1 = run("v", [lowt], V.tensor_copy, blk(T.bw, 0), low.indirect(off(7)))
+        o2 = conv(blk(T.tf, 1), t2, tb[:, 0:20])
+        send(lb[:, 0:20], tb[:, 0:20], "ab", o2)
+        t4 = run("s", [t2, o2], S.activation, blk(T.tf, 2), blk(T.tf, 1).indirect(tb[:, 0:20]), COPY)
+        b2 = run("v", [b1], V.tensor_copy, blk(T.bw, 1), blk(T.bw, 0).indirect(off(7)))
+        o4 = conv(blk(T.tf, 2), t4, tc[:, 0:20])
+        send(lc[:, 0:20], tc[:, 0:20], "ac", o4)
+        left += 5 * ne
         b3 = run("s", [b2], S.activation, blk(T.bw, 2), blk(T.bw, 1).indirect(off(6)), COPY)
-        sg = run("s", [sfull], S.activation, T.sg[:], T.sf[:], COPY)
-        o4 = conv(blk(T.tf, 2), t4, tb[:, 20:40], 160.25)
-        need("g", o4)
-        send(lu[:, 0:40], tb[:, 0:40], "ab%d" % i)
-        left += 4 * ne
-        if i == 0:
-            d1 = run("v", [k_dj, m1], V.tensor_scalar, T.e1[:, 3:515:4], T.dj[:], 0.0, 1.0, A.is_equal, A.mult)
-            for b in range(4):
-                qe1 = run("v", [d1], V.quantize_mx, T.qe1[:, 128 * b:128 * b + 128], T.se1[:, 128 * b:128 * b + 128], T.e1[:, 3 - b:515 - b])
-        ro = conv(blk(T.bw, 2), b3, off(8), 160.25)
+        ro = conv(blk(T.bw, 2), b3, off(8))
 
         fbank = [T.psf[:, 0:C], T.psf[:, 512:512 + C], T.psf[:, 1024:1024 + C], T.pss[:, 0:C]]
-        ff = [run("t", [qe1, sfull], TE.matmul_mx, fbank[b], T.qe1[:, 128 * b:128 * b + 128], T.se1[:, 128 * b:128 * b + 128],
-                  q[:, 0:C], s[:, 0:C], True, True) for b in range(4)]
+        ff = [run("t", [qe1, sf[1]], TE.matmul_mx, fbank[b], mov(T.qe1, b), mov(T.se1, b), q[:, 0:C], s[:, 0:C], True, True) for b in range(4)]
 
-        at, ab = ("at%d" % i, na), ("ab%d" % i, na)
-        zs = [run("s", [at, fw[b]], S.activation, blk(T.tmp, b - 2), blk(T.fw, b).indirect(lt[:, 0:20]), COPY) for b in (2, 3)]
-        z1 = [run("v", [at, fw[b], fd[b]], V.tensor_tensor, blk(T.z1, b), blk(T.fw, b).indirect(lt[:, 0:20]), blk(T.fd, b), A.add) for b in (0, 1)]
+        at, ab, ac = [("%s%d" % (k, i), na) for k in ("at", "ab", "ac")]
+        zs = [run("s", [at, fw[b]], S.activation, blk(T.tmp, b - 2), blk(T.fw, b).indirect(la[:, 0:20]), COPY) for b in (2, 3)]
+        z1 = [run("v", [at, fw[b], fd[b]], V.tensor_tensor, blk(T.z1, b), blk(T.fw, b).indirect(la[:, 0:20]), blk(T.fd, b), A.add) for b in (0, 1)]
         z1 += [run("v", [zs[b - 2]], V.tensor_tensor, blk(T.z1, b), blk(T.tmp, b - 2), T.psa[:, 512 * b:512 * b + C], A.add) for b in (2, 3)]
         d1 = [run("s", [z1[b]], S.activation, blk(T.d1, b), blk(T.z1, b), COPY) for b in range(4)]
-        z2 = [run("v", [ab, z1[b], d1[b]], V.tensor_tensor, blk(T.z2, b), blk(T.z1, b).indirect(lu[:, 0:20]), blk(T.d1, b), A.add) for b in range(4)]
+        z2 = [run("v", [ab, z1[b], d1[b]], V.tensor_tensor, blk(T.z2, b), blk(T.z1, b).indirect(lb[:, 0:20]), blk(T.d1, b), A.add) for b in range(4)]
         d2 = [run("s", [z2[b]], S.activation, blk(T.d2, b), blk(T.z2, b), COPY) for b in range(4)]
-        z3 = [run("v", [z2[b], d2[b]], V.tensor_tensor, T.z3[:, b:1280:4], blk(T.z2, b).indirect(lu[:, 20:40]), blk(T.d2, b), A.add) for b in range(4)]
+        z3 = [run("v", [ac, z2[b], d2[b]], V.tensor_tensor, T.z3[:, b:1280:4], blk(T.z2, b).indirect(lc[:, 0:20]), blk(T.d2, b), A.add) for b in range(4)]
         tz = run("v", z3, V.quantize_mx, T.qz[:, 0:C], T.sz[:, 0:C], T.z3[:])
         fo = [run("s", [ff[b]], S.activation, blk(T.fo, b), fbank[b], COPY) for b in range(4)]
-        f3 = fo[3]
 
-        hh = [run("t", [tz, ("ldw", 32), fw[3]], TE.matmul_mx, T.psa[:, 512 * b:512 * b + C], T.wq[:, 128 * b:128 * b + 128],
-                  T.wsq[:, 128 * b:128 * b + 128], T.qz[:, 0:C], T.sz[:, 0:C], True, True) for b in range(4)]
+        hh = [run("t", [tz, ("ldw", 32), fw[3]], TE.matmul_mx, T.psa[:, 512 * b:512 * b + C], mov(T.wq, b), mov(T.wsq, b),
+                  T.qz[:, 0:C], T.sz[:, 0:C], True, True) for b in range(4)]
         hw = [run("s", [hh[b]], S.activation, blk(T.hw, b), T.psa[:, 512 * b:512 * b + C], COPY, scale=0.03125) for b in range(4)]
 
         a = run("v", [ro, sg], V.tensor_tensor, T.fl[:], T.sf[:, 0:C].indirect(off(8)), T.sg[:, 0:C], A.is_gt)
-        a = run("v", [a], V.tensor_tensor_scan, T.sca[:], T.kk[:], T.fl[:], 0.0, A.mult, A.add)
-        a = run("v", [a], V.tensor_scalar, T.ew[:], w20(T.sca), T.scl[:, 0:1], 0.5, A.mult, A.is_gt)
-        a = run("v", [a], V.tensor_tensor, T.ed[:], T.ew[:], T.dw[:], A.mult)
-        l0 = run("v", [a], V.tensor_tensor, T.l0w[:], T.l0w[:], T.ed[:], A.add)
-        l1 = run("v", [a], V.tensor_tensor, T.l1w[:], T.l1w[:], T.ed[:], A.subtract)
+        a = scan(T.fl[:], [a])
+        e = run("v", [a], V.tensor_scalar, T.ew[:], w20(T.sca), T.thr[:, 0:1], T.inv[:, 0:1], A.is_gt, A.mult)
+
+        tx = []
+        for b in range(4):
+            tx.append(run("v", [hw[b], fo[b], tt], V.tensor_tensor, T.xt[:, b:1280:4], blk(T.hw, b).indirect(ta[:, 0:20]), blk(T.fo, b), A.add))
+            if i == 2 and b == 0:
+                e = run("v", [e], V.tensor_tensor, T.ed[:], T.ew[:], T.dw[:], A.mult)
+            if i == 2 and b == 1:
+                l0 = run("v", [e], V.tensor_tensor, T.l0w[:], T.l0w[:], T.ed[:], A.add)
+                l1 = run("v", [e], V.tensor_tensor, T.l1w[:], T.l1w[:], T.ed[:], A.subtract)
+            if i == 2 and b == 2:
+                l0 = run("v", [l0], V.tensor_copy, T.l0o[:], T.l0w[:])
+                l1 = run("v", [l1], V.tensor_copy, T.l1o[:], T.l1w[:])
+                lsd = [run("s", [k_if, t], S.activation, T.lsf[:, C * h:C * h + C], T.iof[:, 0:C].indirect(o[:, 0:20]), COPY)
+                       for h, t, o in ((0, l0, T.l0o), (1, l1, T.l1o))]
+        tq = quant(T.xt, i + 1, [tx, tx])
         if i < 2:
-            dw = run("v", [l0, l1], V.tensor_tensor, T.dw[:], T.l1w[:], T.l0w[:], A.subtract)
-        else:
-            a = run("v", [l0], V.tensor_copy, T.l0o[:], T.l0w[:])
-            b = run("v", [l1], V.tensor_copy, T.l1o[:], T.l1w[:])
-            a = run("s", [a, k_if], S.activation, T.lsf[:, 0:C], T.iof[:, 0:C].indirect(T.l0o[:, 0:20]), COPY)
-            lsd = run("s", [b, k_if], S.activation, T.lsf[:, C:2 * C], T.iof[:, 0:C].indirect(T.l1o[:, 0:20]), COPY)
+            e = run("v", [e], V.tensor_tensor, T.ed[:], T.ew[:], T.dw[:], A.mult)
+            l0 = run("v", [e], V.tensor_tensor, T.l0w[:], T.l0w[:], T.ed[:], A.add)
+            eg = run("v", [e], V.tensor_scalar, T.eg[:], T.ed[:], T.scm[:, 0:1], None, A.mult)
 
-        tx = [run("v", [hw[b], fo[b], tt], V.tensor_tensor, T.xt[:, b:1280:4], blk(T.hw, b).indirect(to[:, 0:20]), blk(T.fo, b), A.add) for b in range(4)]
-        tq = run("v", tx, V.quantize_mx, T["q%d" % (i + 1)][:, 0:C], T["s%d" % (i + 1)][:, 0:C], T.xt[:])
-        if i == 0:
-            qv = run("v", [("ldv", 16)], V.quantize_mx, T.qv[:, 0:128], T.sv[:, 0:128], T.vin[:])
-
-    need("y", lsd)
+    need("y", *lsd)
     g.sync.dma_start(T.ls[:, :], T.lsf[0:128:16, :]).then_inc(T.sem.sto, 16)
-    yy = [run("t", [tq, qv, hw[3]], TE.matmul_mx, T.psa[:, 512 * h:512 * h + 160], T.qv[:, 0:128], T.sv[:, 0:128],
-              T.q3[:, 160 * h:160 * h + 160], T.s3[:, 160 * h:160 * h + 160], True, True) for h in (0, 1)]
-    need("y", tq)
+    need("y", *tq)
     g.sync.dma_start(T.oc[:, :], T.q3[:, 0:C].bitcast(dt.uint8)).then_inc(T.sem.sto, 16)
-    ya = run("v", [yy[0]], V.tensor_copy, T.yf[:, 0:160], T.psa[:, 0:160])
-    yb = run("s", [yy[1]], S.activation, T.yf[:, 160:320], T.psa[:, 512:672], COPY)
+    yy = [run("t", [tq[h], qv, hw[3]], TE.matmul_mx, T.psa[:, 512 * h:512 * h + H], T.qv[:, 0:128], T.sv[:, 0:128],
+              T.q3[:, H * h:H * h + H], T.s3[:, H * h:H * h + H], True, True) for h in (0, 1)]
+    ya = run("v", [yy[0]], V.tensor_copy, T.yf[:, 0:H], T.psa[:, 0:H])
+    yb = run("s", [yy[1]], S.activation, T.yf[:, H:C], T.psa[:, 512:512 + H], COPY)
     need("y", ya)
-    g.sync.dma_start(T.y[:, 0:160], T.yf[:, 0:160]).then_inc(T.sem.sto, 16)
-    need("s", yb, tq)
-    g.scalar.dma_start(T.y[:, 160:320], T.yf[:, 160:320]).then_inc(T.sem.stc, 16)
+    g.sync.dma_start(T.y[:, 0:H], T.yf[:, 0:H]).then_inc(T.sem.sto, 16)
+    need("s", yb)
+    g.scalar.dma_start(T.y[:, H:C], T.yf[:, H:C]).then_inc(T.sem.stc, 16)
     for k in range(4):
-        e, sem = (g.sync, T.sem.sto) if k < 2 else (g.scalar, T.sem.stc)
-        e.dma_start(T.osc[4 * k:4 * k + 4, :], T.s3[32 * k:32 * k + 4, 0:C]).then_inc(sem, 16)
-    need("g", ("cv", cnt["v"]), ("cs", cnt["s"]), ("ct", cnt["t"]), ("cg", cnt["g"]), ("left", left), ("sto", 80), ("stc", 48))
+        g.sync.dma_start(T.osc[4 * k:4 * k + 4, :], T.s3[32 * k:32 * k + 4, 0:C]).then_inc(T.sem.sto, 16)
+    need("g", ("cv", cnt["v"]), ("cs", cnt["s"]), ("ct", cnt["t"]), ("cg", cnt["g"]), ("left", left), ("sto", 112), ("stc", 16))

@@ -16,8 +16,8 @@ def _sb(dtype, **kw):
 _sb(BF, xin=1280, uin=512, vin=512, e8=516, e1=516, iot=320, tpos=320, n0=320, n1=320, kk=320, sca=320, mm=320,
     aw=320 * 8, low=320 * 9, tf=960, bw=960, fw=1280, fo=1280, hw=1280, z1=1280, z2=1280, z3=1280, xt=1280, tmp=640,
     fl=320, ld=320 * 9, fd=640, d1=1280, d2=1280)
-_sb(F32, iof=320, dj=128, m16=20, kf=1, k1=1, scl=1, scm=1, thr=1, inv=1, cw=20, cb=20, sf=320, sg=320, l0w=20, l1w=20,
-    dw=20, tp=20, pw=20, dcp=20, ew=20, ed=20, eg=20, tw=20, lsf=640, yf=320)
+_sb(F32, iof=320, dj=128, m16=20, kf=1, k1=1, scl=1, scm=1, thr=1, inv=1, cw=20, cb=20, sf=320, l0w=20, l1w=20,
+    dw=20, ss=20, sg=320, tp=20, pw=20, dcp=20, ew=20, ed=20, eg=20, tw=20, lsf=640, yf=320)
 _sb(I32, lai=20, lbi=20, pi=1, ki=1, lwi=20)
 _sb(U16, uo=8, offs=180, l0o=20, l1o=20)
 _sb("float8_e4m3fn_x4", wq=512, qu=128, qup=128, qv=128, qe8=512, qe1=512, qz=320)
@@ -94,7 +94,6 @@ def rank_program(g, core, T, topo):
     k_io = run("g", [], g.iota, T.iot[:], [[1, C]], -160, 0, **SMALL)
 
     m8 = run("v", [], V.memset, T.e8[:], 0.0)
-    m1 = run("v", [], V.memset, T.e1[:], 0.0)
     uo = run("v", [k_m16], V.tensor_copy, T.uo[:], T.m16[:, 0:8])
     ki = run("v", [k_pi], V.tensor_scalar, T.ki[:], T.pi[:], 15, None, A.bitwise_and)
     kf = run("v", [ki], V.tensor_copy, T.kf[:], T.ki[:])
@@ -112,14 +111,9 @@ def rank_program(g, core, T, topo):
     run("v", [sc], V.tensor_scalar, T.scm[:], T.scl[:], -2.0, None, A.mult)
     run("v", [b], V.tensor_scalar, T.thr[:], T.inv[:], 0.5, None, A.mult)
 
-    def diagonal(e, q, s, dep):
-        return [run("v", [dep], V.quantize_mx, mov(q, b), mov(s, b), e[:, 3 - b:515 - b]) for b in range(4)][3]
-
-    qe8 = diagonal(T.e8, T.qe8, T.se8, d8)
-
     a = run("v", [("ldu", 16)], V.quantize_mx, T.qu[:, 0:128], T.su[:, 0:128], T.uin[:])
-    run("v", [a, uo], V.tensor_copy, T.qup[:, 0:128].bitcast(dt.uint32), T.qu[:, 0:128].bitcast(dt.uint32).indirect(T.uo[:, 0:8]))
-    qup = run("v", [a, uo], V.tensor_copy, T.sup[:, 0:128], T.su[:, 0:128].indirect(T.uo[:, 0:8]))
+    qup = run("v", [a, uo], V.tensor_copy, T.qup[:, 0:128].bitcast(dt.uint32), T.qu[:, 0:128].bitcast(dt.uint32).indirect(T.uo[:, 0:8]))
+    qus = run("s", [a, uo], S.activation, T.sup[:, 0:128], T.su[:, 0:128].indirect(T.uo[:, 0:8]), COPY)
 
     def quant(tile, i, deps):
         return [run("v", deps[h], V.quantize_mx, T["q%d" % i][:, H * h:H * h + H], T["s%d" % i][:, H * h:H * h + H],
@@ -129,6 +123,7 @@ def rank_program(g, core, T, topo):
     l0 = run("v", [("ldl", 32)], V.tensor_scalar, T.l0w[:], T.lai[:], 0.25, None, A.add)
     l1 = run("v", [("ldl", 32)], V.tensor_scalar, T.l1w[:], T.lbi[:], 0.25, None, A.add)
     a = run("v", [l0, l1], V.tensor_tensor, T.dw[:], T.l1w[:], T.l0w[:], A.subtract)
+    ss = run("v", [l0, l1], V.tensor_tensor, T.ss[:], T.l1w[:], T.l0w[:], A.add)
     dw = run("v", [a, sc], V.tensor_scalar, T.dw[:], T.dw[:], T.scl[:, 0:1], None, A.mult)
 
     def scan(src, deps):
@@ -142,7 +137,6 @@ def rank_program(g, core, T, topo):
         return T.offs[:, 20 * k:20 * k + 20]
 
     left = 0
-    qe1 = None
     for i, d in enumerate(STEP):
         q, s = T["q%d" % i], T["s%d" % i]
         lq, lp = T["lq%d" % i], T["lp%d" % i]
@@ -164,28 +158,26 @@ def rank_program(g, core, T, topo):
             k_if = run("g", [], g.iota, T.iof[:], [[1, C]], 0, 0, **SMALL)
 
         sbank = [T.pss[:, 0:H], T.psf[:, 0:H]]
-        ts = [run("t", [tq[h], qup], TE.matmul_mx, sbank[h], T.qup[:, 0:128], T.sup[:, 0:128],
+        ts = [run("t", [tq[h], qup, qus], TE.matmul_mx, sbank[h], T.qup[:, 0:128], T.sup[:, 0:128],
                   q[:, H * h:H * h + H], s[:, H * h:H * h + H], True, True) for h in (0, 1)]
-        m = [run("v", [ts[h]], V.tensor_scalar, T.mm[:, H * h:H * h + H], sbank[h], 0.0, None, A.is_lt) for h in (0, 1)]
-        if i:
-            dw = run("v", [eg], V.tensor_tensor, T.dw[:], T.dw[:], T.eg[:], A.add)
-        a = run("v", m + [kk], V.tensor_tensor_scan, T.sca[:], T.kk[:], T.mm[:], 0.0, A.mult, A.add)
+        m = []
+        for h in (0, 1):
+            half = slice(H * h, H * h + H)
+            m.append(run("v", [ts[h]], V.tensor_scalar, T.mm[:, half], sbank[h], 0.0, None, A.is_lt))
+            if i and h:
+                dw = run("v", [eg], V.tensor_tensor, T.dw[:], T.dw[:], T.eg[:], A.add)
+            a = run("v", [m[h], kk], V.tensor_tensor_scan, T.sca[:, half], T.kk[:, half], T.mm[:, half], 0.0, A.mult, A.add)
         a = run("v", [a, dw], V.tensor_tensor, T.tp[:], w20(T.sca), T.dw[:], A.mult)
         pw = run("v", [a, l0], V.tensor_tensor, T.pw[:], T.tp[:], T.l0w[:], A.add)
         o = run("v", [pw], V.tensor_copy, off(0), T.pw[:])
         sf = [run("s", [m[h]], S.activation, T.sf[:, H * h:H * h + H], sbank[h], COPY) for h in (0, 1)]
         dcp = run("v", [pw, cb], V.tensor_tensor, T.dcp[:], T.cb[:], T.pw[:], A.subtract)
-        if i == 0:
-            qe1 = diagonal(T.e1, T.qe1, T.se1, run("v", [k_dj, m1], V.tensor_scalar, T.e1[:, 3:515:4], T.dj[:], 0.0, 1.0, A.is_equal, A.mult))
-
-        if i:
-            run("v", [e], V.tensor_tensor, T.l1w[:], T.l1w[:], T.ed[:], A.subtract)
-        if i == 1:
-            qv = run("v", [("ldv", 16)], V.quantize_mx, T.qv[:, 0:128], T.sv[:, 0:128], T.vin[:])
 
         ak = run("s", [o, k_io], S.activation, blk(T.aw, 0), T.iot[:, 0:C].indirect(off(0)), COPY)
         low, lowt = blk(T.aw, 0), ak
-        dup = run("v", [ak], V.tensor_copy, blk(T.ld, 0), low)
+        dup = run("v", [o, k_io], V.tensor_copy, blk(T.ld, 0), T.iot[:, 0:C].indirect(off(0)))
+        if i == 0:
+            qe8 = [run("v", [d8], V.quantize_mx, mov(T.qe8, b), mov(T.se8, b), T.e8[:, 3 - b:515 - b]) for b in range(4)][3]
         for k in range(7):
             an = run("s", [ak, o], S.activation, blk(T.aw, k + 1), blk(T.aw, k).indirect(off(k)), COPY)
             lowt = run("v", [lowt, o, ak, dup], V.tensor_tensor, blk(T.low, k), low.indirect(off(k)), blk(T.ld, k), A.min)
@@ -195,8 +187,7 @@ def rank_program(g, core, T, topo):
             ak = an
         lowt = run("v", [lowt, o, dup], V.tensor_tensor, blk(T.low, 7), low.indirect(off(7)), blk(T.ld, 7), A.min)
         low = blk(T.low, 7)
-        dup = run("v", [lowt], V.tensor_copy, blk(T.ld, 8), low)
-        lowt = run("v", [lowt, dup], V.tensor_tensor, blk(T.low, 8), low.indirect(off(6)), blk(T.ld, 8), A.min)
+        lowt = run("v", [lowt], V.tensor_tensor, blk(T.low, 8), low.indirect(off(6)), blk(T.ld, 7), A.min)
         low = blk(T.low, 8)
         a = conv(low, lowt, T.lwi[:])
         a = run("v", [a, cw], V.tensor_tensor, T.ew[:], T.lwi[:], T.cw[:], A.is_equal)
@@ -207,25 +198,27 @@ def rank_program(g, core, T, topo):
 
         f8 = [run("t", [("aq%d" % i, 2 * na), qe8, sf[1]], TE.matmul_mx, T.psa[:, 512 * b:512 * b + C], mov(T.qe8, b), mov(T.se8, b),
                   lq[:, 0:C], lp[:, 0:C], True, True) for b in range(4)]
-        fw = [run("s", [f8[b]], S.activation, blk(T.fw, b), T.psa[:, 512 * b:512 * b + C], COPY) for b in range(4)]
-        fd = [run("v", [fw[b]], V.tensor_copy, blk(T.fd, b), blk(T.fw, b)) for b in (0, 1)]
+        fw = []
+        for b in range(4):
+            if b == 3:
+                b1 = run("s", [lowt], S.activation, blk(T.bw, 0), low.indirect(off(7)), COPY)
+            fw.append(run("s", [f8[b]], S.activation, blk(T.fw, b), T.psa[:, 512 * b:512 * b + C], COPY))
 
         t1 = run("s", [tt], S.activation, blk(T.tf, 0), T.iot[:, 0:C].indirect(ta[:, 0:20]), COPY)
         t2 = run("s", [t1], S.activation, blk(T.tf, 1), blk(T.tf, 0).indirect(ta[:, 0:20]), COPY)
-        sg = run("s", [sf[1]], S.activation, T.sg[:], T.sf[:], COPY)
-        b1 = run("v", [lowt], V.tensor_copy, blk(T.bw, 0), low.indirect(off(7)))
+        b2 = run("v", [b1], V.tensor_copy, blk(T.bw, 1), blk(T.bw, 0).indirect(off(7)))
+        b3 = run("v", [b2], V.tensor_copy, blk(T.bw, 2), blk(T.bw, 1).indirect(off(6)))
         o2 = conv(blk(T.tf, 1), t2, tb[:, 0:20])
         send(lb[:, 0:20], tb[:, 0:20], "ab", o2)
         t4 = run("s", [t2, o2], S.activation, blk(T.tf, 2), blk(T.tf, 1).indirect(tb[:, 0:20]), COPY)
-        b2 = run("v", [b1], V.tensor_copy, blk(T.bw, 1), blk(T.bw, 0).indirect(off(7)))
+        ro = conv(blk(T.bw, 2), b3, off(8))
+        fd = [run("v", [fw[b]], V.tensor_copy, blk(T.fd, b), blk(T.fw, b)) for b in (0, 1)]
+        sg = run("s", [ro, sf[1]], S.activation, T.sg[:], T.sf[:, 0:C].indirect(off(8)), COPY)
         o4 = conv(blk(T.tf, 2), t4, tc[:, 0:20])
         send(lc[:, 0:20], tc[:, 0:20], "ac", o4)
         left += 5 * ne
-        b3 = run("s", [b2], S.activation, blk(T.bw, 2), blk(T.bw, 1).indirect(off(6)), COPY)
-        ro = conv(blk(T.bw, 2), b3, off(8))
-
-        fbank = [T.psf[:, 0:C], T.psf[:, 512:512 + C], T.psf[:, 1024:1024 + C], T.pss[:, 0:C]]
-        ff = [run("t", [qe1, sf[1]], TE.matmul_mx, fbank[b], mov(T.qe1, b), mov(T.se1, b), q[:, 0:C], s[:, 0:C], True, True) for b in range(4)]
+        if i == 0:
+            qv = run("v", [("ldv", 16)], V.quantize_mx, T.qv[:, 0:128], T.sv[:, 0:128], T.vin[:])
 
         at, ab, ac = [("%s%d" % (k, i), na) for k in ("at", "ab", "ac")]
         zs = [run("s", [at, fw[b]], S.activation, blk(T.tmp, b - 2), blk(T.fw, b).indirect(la[:, 0:20]), COPY) for b in (2, 3)]
@@ -235,15 +228,24 @@ def rank_program(g, core, T, topo):
         z2 = [run("v", [ab, z1[b], d1[b]], V.tensor_tensor, blk(T.z2, b), blk(T.z1, b).indirect(lb[:, 0:20]), blk(T.d1, b), A.add) for b in range(4)]
         d2 = [run("s", [z2[b]], S.activation, blk(T.d2, b), blk(T.z2, b), COPY) for b in range(4)]
         z3 = [run("v", [ac, z2[b], d2[b]], V.tensor_tensor, T.z3[:, b:1280:4], blk(T.z2, b).indirect(lc[:, 0:20]), blk(T.d2, b), A.add) for b in range(4)]
-        tz = run("v", z3, V.quantize_mx, T.qz[:, 0:C], T.sz[:, 0:C], T.z3[:])
-        fo = [run("s", [ff[b]], S.activation, blk(T.fo, b), fbank[b], COPY) for b in range(4)]
+        tz = [run("v", z3, V.quantize_mx, T.qz[:, H * h:H * h + H], T.sz[:, H * h:H * h + H], T.z3[:, 4 * H * h:4 * H * h + 4 * H]) for h in (0, 1)]
 
-        hh = [run("t", [tz, ("ldw", 32), fw[3]], TE.matmul_mx, T.psa[:, 512 * b:512 * b + C], mov(T.wq, b), mov(T.wsq, b),
-                  T.qz[:, 0:C], T.sz[:, 0:C], True, True) for b in range(4)]
-        hw = [run("s", [hh[b]], S.activation, blk(T.hw, b), T.psa[:, 512 * b:512 * b + C], COPY, scale=0.03125) for b in range(4)]
+        fbank = [T.psf[:, 512:512 + C], T.psf[:, 1024:1024 + C]]
+        ff, fo = [], []
+        for b in range(4):
+            ff.append(run("t", [qe8] + fo[b - 2:b - 1], TE.matmul_mx, fbank[b % 2], mov(T.qe8, b), mov(T.se8, b), q[:, 0:C], s[:, 0:C], True, True))
+            fo.append(run("s", [ff[b]], S.activation, blk(T.fo, b), fbank[b % 2], COPY, scale=8.0))
 
-        a = run("v", [ro, sg], V.tensor_tensor, T.fl[:], T.sf[:, 0:C].indirect(off(8)), T.sg[:, 0:C], A.is_gt)
-        a = scan(T.fl[:], [a])
+        hbank = [T.psa[:, 0:H], T.psf[:, 512:512 + H]]
+        hh = [run("t", [tz[h], ("ldw", 32), fw[3], fo[2]], TE.matmul_mx, hbank[h], mov(T.wq, 0), mov(T.wsq, 0),
+                  T.qz[:, H * h:H * h + H], T.sz[:, H * h:H * h + H], True, True) for h in (0, 1)]
+        hh += [run("t", [tz[1]], TE.matmul_mx, T.psa[:, 512 * b:512 * b + C], mov(T.wq, b), mov(T.wsq, b),
+                   T.qz[:, 0:C], T.sz[:, 0:C], True, True) for b in (1, 2, 3)]
+        hw = [run("s", [hh[h]], S.activation, T.hw[:, H * h:H * h + H], hbank[h], COPY, scale=0.03125) for h in (0, 1)][1:]
+        hw += [run("s", [hh[b + 1]], S.activation, blk(T.hw, b), T.psa[:, 512 * b:512 * b + C], COPY, scale=0.03125) for b in (1, 2, 3)]
+
+        a = [run("v", [sg], V.tensor_tensor, T.fl[:, H * h:H * h + H], T.sg[:, H * h:H * h + H], sbank[h], A.is_gt) for h in (0, 1)]
+        a = scan(T.fl[:], a)
         e = run("v", [a], V.tensor_scalar, T.ew[:], w20(T.sca), T.thr[:, 0:1], T.inv[:, 0:1], A.is_gt, A.mult)
 
         tx = []
@@ -253,8 +255,8 @@ def rank_program(g, core, T, topo):
                 e = run("v", [e], V.tensor_tensor, T.ed[:], T.ew[:], T.dw[:], A.mult)
             if i == 2 and b == 1:
                 l0 = run("v", [e], V.tensor_tensor, T.l0w[:], T.l0w[:], T.ed[:], A.add)
-                l1 = run("v", [e], V.tensor_tensor, T.l1w[:], T.l1w[:], T.ed[:], A.subtract)
             if i == 2 and b == 2:
+                l1 = run("v", [l0, ss], V.tensor_tensor, T.l1w[:], T.ss[:], T.l0w[:], A.subtract)
                 l0 = run("v", [l0], V.tensor_copy, T.l0o[:], T.l0w[:])
                 l1 = run("v", [l1], V.tensor_copy, T.l1o[:], T.l1w[:])
                 lsd = [run("s", [k_if, t], S.activation, T.lsf[:, C * h:C * h + C], T.iof[:, 0:C].indirect(o[:, 0:20]), COPY)

from concourse.mybir import dt, AluOpType, ActivationFunctionType

C = 320
H = 160
STEP = [1, 2, 4]
BF, F32, I32, U16 = "bfloat16", "float32", "int32", "uint16"

SCRATCH = {}


def _sb(dtype, **kw):
    for k, n in kw.items():
        SCRATCH[k] = ("sbuf", [128, n], dtype)


_sb(BF, xin=1280, uin=512, vin=512, e8=516, e1=516, iot=320, tpos=320, n0=320, n1=320, kk=320, sca=320, mm=320,
    aw=320 * 8, low=320 * 9, tf=960, bw=960, fw=1280, fo=1280, hw=1280, z1=1280, z2=1280, z3=1280, xt=1280, tmp=640,
    fl=320, ld=320 * 9, fd=640, d1=1280, d2=1280)
_sb(F32, iof=320, dj=128, m16=20, kf=1, k1=1, scl=1, scm=1, thr=1, inv=1, cw=20, cb=20, sf=320, l0w=20, l1w=20,
    dw=20, ss=20, sg=320, tp=20, pw=20, dcp=20, ew=20, ed=20, eg=20, tw=20, lsf=640, yf=320)
_sb(I32, lai=20, lbi=20, pi=1, ki=1, lwi=20)
_sb(U16, uo=8, offs=180, l0o=20, l1o=20)
_sb("float8_e4m3fn_x4", wq=512, qu=128, qup=128, qv=128, qe8=512, qe1=512, qz=320)
_sb("uint8", wsq=512, su=128, sup=128, sv=128, se8=512, se1=512, sz=320)
for _i in range(4):
    SCRATCH["q%d" % _i] = ("sbuf", [128, C], "float8_e4m3fn_x4")
    SCRATCH["s%d" % _i] = ("sbuf", [128, C], "uint8")
for _i in range(3):
    SCRATCH["lq%d" % _i] = ("sbuf", [128, C], "float8_e4m3fn_x4")
    SCRATCH["lp%d" % _i] = ("sbuf", [128, C], "uint8")
    for _k in ("ta", "tb", "tc", "la_", "lb_", "lc_"):
        SCRATCH["%s%d" % (_k, _i)] = ("sbuf", [128, 20], U16)
SCRATCH["psa"] = ("psum", [128, 2048], F32)
SCRATCH["psf"] = ("psum", [128, 1536], F32)
SCRATCH["pss"] = ("psum", [128, 512], F32)

SEMAPHORES = ["cv", "cs", "ct", "cg", "left", "ldx", "ldy", "ldu", "ldv", "ldl", "ldw", "sto", "stc"]
SEMAPHORES += ["%s%d" % (k, i) for k in ("aq", "at", "ab", "ac") for i in range(3)]


def rank_program(g, core, T, topo):
    rank = T.rank_of(core)
    if rank is None:
        return
    N = len(T.cores)
    A = AluOpType
    COPY = ActivationFunctionType.Copy
    eng = {"v": g.vector, "s": g.scalar, "t": g.tensor, "g": g, "y": g.sync}
    cnt = {"v": 0, "s": 0, "t": 0, "g": 0}
    seen = {}

    def need(q, *toks):
        most = {}
        for name, n in toks:
            most[name] = max(n, most.get(name, 0))
        for name, n in most.items():
            if seen.get((q, name), 0) < n:
                eng[q].wait_ge(T.sem[name], n)
                seen[(q, name)] = n

    def run(q, deps, fn, *a, **kw):
        need(q, *deps)
        ins = fn(*a, **kw)
        cnt[q] += 1
        ins.then_inc(T.sem["c" + q], 1)
        return ("c" + q, cnt[q])

    V, S, TE = g.vector, g.scalar, g.tensor

    def w20(buf):
        return buf[:, 15:C:16]

    def blk(buf, b):
        return buf[:, C * b:C * b + C]

    def mov(buf, b):
        return buf[:, 128 * b:128 * b + 128]

    g.sync.dma_start(T.xin[:, 0:640], T.x[:, 0:640]).then_inc(T.sem.ldx, 16)
    g.scalar.dma_start(T.uin[:], T.u[:, :]).then_inc(T.sem.ldu, 16)
    g.scalar.dma_start(T.xin[:, 640:1280], T.x[:, 640:1280]).then_inc(T.sem.ldy, 16)
    g.sync.dma_start(T.lai[:], T.la[:, :]).then_inc(T.sem.ldl, 16)
    g.sync.dma_start(T.lbi[:], T.lb[:, :]).then_inc(T.sem.ldl, 16)
    need("y", ("ldx", 16), ("ldy", 16))
    g.sync.dma_start(T.wq[:, 0:512].bitcast(dt.uint8), T.wc[:, :]).then_inc(T.sem.ldw, 16)
    g.sync.dma_start(T.wsq[:, 0:512], T.ws[:, :]).then_inc(T.sem.ldw, 16)
    g.sync.dma_start(T.vin[:], T.v[:, :]).then_inc(T.sem.ldv, 16)

    SMALL = {"allow_small_or_imprecise_dtypes": True}
    k_m16 = run("g", [], g.iota, T.m16[:], [[16, 20]], 0, 0, **SMALL)
    k_pi = run("g", [], g.iota, T.pi[:], [[0, 1]], 0, 1)
    k_tp = run("g", [], g.iota, T.tpos[:], [[0, 20], [1, 16]], 0, 0, **SMALL)
    k_dj = run("g", [], g.iota, T.dj[:], [[1, 128]], 0, -1, **SMALL)
    k_io = run("g", [], g.iota, T.iot[:], [[1, C]], -160, 0, **SMALL)

    m8 = run("v", [], V.memset, T.e8[:], 0.0)
    uo = run("v", [k_m16], V.tensor_copy, T.uo[:], T.m16[:, 0:8])
    ki = run("v", [k_pi], V.tensor_scalar, T.ki[:], T.pi[:], 15, None, A.bitwise_and)
    kf = run("v", [ki], V.tensor_copy, T.kf[:], T.ki[:])
    k1 = run("v", [kf], V.tensor_scalar, T.k1[:], T.kf[:], 1.0, None, A.add)
    a = run("v", [kf], V.tensor_scalar, T.scl[:], T.kf[:], 15.0, 1.0 - 2.0 ** -15, A.is_equal, A.mult)
    b = run("v", [kf], V.tensor_scalar, T.inv[:], T.kf[:], 15.0, 1.0 - 2.0 ** 15, A.is_equal, A.mult)
    sc = run("v", [a], V.tensor_scalar, T.scl[:], T.scl[:], 2.0 ** -15, None, A.add)
    b = run("v", [b], V.tensor_scalar, T.inv[:], T.inv[:], 2.0 ** 15, None, A.add)
    n0 = run("v", [k_tp, kf], V.tensor_scalar, T.n0[:], T.tpos[:], T.kf[:, 0:1], None, A.not_equal)
    n1 = run("v", [k_tp, k1], V.tensor_scalar, T.n1[:], T.tpos[:], T.k1[:, 0:1], 2.0 ** 15, A.is_equal, A.mult)
    cw = run("v", [k_m16, kf], V.tensor_scalar, T.cw[:], T.m16[:], T.kf[:, 0:1], None, A.add)
    cb = run("v", [k_m16, kf], V.tensor_scalar, T.cb[:], T.m16[:], T.kf[:, 0:1], 0.25, A.add, A.add)
    kk = run("v", [n0, n1], V.tensor_tensor, T.kk[:], T.n0[:], T.n1[:], A.max)
    d8 = run("v", [k_dj, m8], V.tensor_scalar, T.e8[:, 3:515:4], T.dj[:], 0.0, 0.125, A.is_equal, A.mult)
    run("v", [sc], V.tensor_scalar, T.scm[:], T.scl[:], -2.0, None, A.mult)
    run("v", [b], V.tensor_scalar, T.thr[:], T.inv[:], 0.5, None, A.mult)

    a = run("v", [("ldu", 16)], V.quantize_mx, T.qu[:, 0:128], T.su[:, 0:128], T.uin[:])
    qup = run("v", [a, uo], V.tensor_copy, T.qup[:, 0:128].bitcast(dt.uint32), T.qu[:, 0:128].bitcast(dt.uint32).indirect(T.uo[:, 0:8]))
    qus = run("s", [a, uo], S.activation, T.sup[:, 0:128], T.su[:, 0:128].indirect(T.uo[:, 0:8]), COPY)

    def quant(tile, i, deps):
        return [run("v", deps[h], V.quantize_mx, T["q%d" % i][:, H * h:H * h + H], T["s%d" % i][:, H * h:H * h + H],
                    tile[:, 4 * H * h:4 * H * h + 4 * H]) for h in (0, 1)]

    tq = quant(T.xin, 0, [[("ldx", 16)], [("ldy", 16)]])
    l0 = run("v", [("ldl", 32)], V.tensor_scalar, T.l0w[:], T.lai[:], 0.25, None, A.add)
    l1 = run("v", [("ldl", 32)], V.tensor_scalar, T.l1w[:], T.lbi[:], 0.25, None, A.add)
    a = run("v", [l0, l1], V.tensor_tensor, T.dw[:], T.l1w[:], T.l0w[:], A.subtract)
    ss = run("v", [l0, l1], V.tensor_tensor, T.ss[:], T.l1w[:], T.l0w[:], A.add)
    dw = run("v", [a, sc], V.tensor_scalar, T.dw[:], T.dw[:], T.scl[:, 0:1], None, A.mult)

    def scan(src, deps):
        return run("v", list(deps) + [kk, ("cv", cnt["v"])], V.tensor_tensor_scan, T.sca[:], T.kk[:], src, 0.0, A.mult, A.add)

    def conv(src, dep, out):
        a = scan(src, [dep])
        return run("v", [a, sc], V.tensor_scalar, out, w20(T.sca), T.scl[:, 0:1], 160.25, A.mult, A.add)

    def off(k):
        return T.offs[:, 20 * k:20 * k + 20]

    left = 0
    for i, d in enumerate(STEP):
        q, s = T["q%d" % i], T["s%d" % i]
        lq, lp = T["lq%d" % i], T["lp%d" % i]
        ta, tb, tc = [T["%s%d" % (k, i)] for k in ("ta", "tb", "tc")]
        la, lb, lc = [T["%s%d" % (k, i)] for k in ("la_", "lb_", "lc_")]
        dst = T.cores[(rank + d) % N]
        src = T.cores[(rank - d) % N]
        rid, pid, _ = topo.addr(dst)
        mask = topo.mask(core, dst)
        ne, na = len(topo.engines(core, dst)), len(topo.engines(src, core))

        def send(out, in_, sem, dep):
            need("g", dep)
            g.remote_dma(out, in_, T.sem["%s%d" % (sem, i)], T.sem.left, pid, rid, mask)

        send(lq[:, 0:C].bitcast(dt.uint8), q[:, 0:C].bitcast(dt.uint8), "aq", tq[1])
        send(lp[:, 0:C], s[:, 0:C], "aq", tq[1])
        if i == 0:
            k_if = run("g", [], g.iota, T.iof[:], [[1, C]], 0, 0, **SMALL)

        sbank = [T.pss[:, 0:H], T.psf[:, 0:H]]
        ts = [run("t", [tq[h], qup, qus], TE.matmul_mx, sbank[h], T.qup[:, 0:128], T.sup[:, 0:128],
                  q[:, H * h:H * h + H], s[:, H * h:H * h + H], True, True) for h in (0, 1)]
        m = []
        for h in (0, 1):
            half = slice(H * h, H * h + H)
            m.append(run("v", [ts[h]], V.tensor_scalar, T.mm[:, half], sbank[h], 0.0, None, A.is_lt))
            if i and h:
                dw = run("v", [eg], V.tensor_tensor, T.dw[:], T.dw[:], T.eg[:], A.add)
            a = run("v", [m[h], kk], V.tensor_tensor_scan, T.sca[:, half], T.kk[:, half], T.mm[:, half], 0.0, A.mult, A.add)
        a = run("v", [a, dw], V.tensor_tensor, T.tp[:], w20(T.sca), T.dw[:], A.mult)
        pw = run("v", [a, l0], V.tensor_tensor, T.pw[:], T.tp[:], T.l0w[:], A.add)
        o = run("v", [pw], V.tensor_copy, off(0), T.pw[:])
        sf = [run("s", [m[h]], S.activation, T.sf[:, H * h:H * h + H], sbank[h], COPY) for h in (0, 1)]
        dcp = run("v", [pw, cb], V.tensor_tensor, T.dcp[:], T.cb[:], T.pw[:], A.subtract)

        ak = run("s", [o, k_io], S.activation, blk(T.aw, 0), T.iot[:, 0:C].indirect(off(0)), COPY)
        low, lowt = blk(T.aw, 0), ak
        dup = run("v", [o, k_io], V.tensor_copy, blk(T.ld, 0), T.iot[:, 0:C].indirect(off(0)))
        if i == 0:
            qe8 = [run("v", [d8], V.quantize_mx, mov(T.qe8, b), mov(T.se8, b), T.e8[:, 3 - b:515 - b]) for b in range(4)][3]
        for k in range(7):
            an = run("s", [ak, o], S.activation, blk(T.aw, k + 1), blk(T.aw, k).indirect(off(k)), COPY)
            lowt = run("v", [lowt, o, ak, dup], V.tensor_tensor, blk(T.low, k), low.indirect(off(k)), blk(T.ld, k), A.min)
            low = blk(T.low, k)
            dup = run("s", [lowt], S.activation, blk(T.ld, k + 1), low, COPY)
            o = conv(blk(T.aw, k + 1), an, off(k + 1))
            ak = an
        lowt = run("v", [lowt, o, dup], V.tensor_tensor, blk(T.low, 7), low.indirect(off(7)), blk(T.ld, 7), A.min)
        low = blk(T.low, 7)
        lowt = run("v", [lowt], V.tensor_tensor, blk(T.low, 8), low.indirect(off(6)), blk(T.ld, 7), A.min)
        low = blk(T.low, 8)
        a = conv(low, lowt, T.lwi[:])
        a = run("v", [a, cw], V.tensor_tensor, T.ew[:], T.lwi[:], T.cw[:], A.is_equal)
        a = run("v", [a, dcp], V.tensor_tensor, T.ed[:], T.ew[:], T.dcp[:], A.mult)
        a = run("v", [a], V.tensor_tensor, T.tw[:], T.ed[:], T.pw[:], A.add)
        tt = run("v", [a], V.tensor_copy, ta[:, 0:20], T.tw[:])
        send(la[:, 0:20], ta[:, 0:20], "at", tt)

        f8 = [run("t", [("aq%d" % i, 2 * na), qe8, sf[1]], TE.matmul_mx, T.psa[:, 512 * b:512 * b + C], mov(T.qe8, b), mov(T.se8, b),
                  lq[:, 0:C], lp[:, 0:C], True, True) for b in range(4)]
        fw = []
        for b in range(4):
            if b == 3:
                b1 = run("s", [lowt], S.activation, blk(T.bw, 0), low.indirect(off(7)), COPY)
            fw.append(run("s", [f8[b]], S.activation, blk(T.fw, b), T.psa[:, 512 * b:512 * b + C], COPY))

        t1 = run("s", [tt], S.activation, blk(T.tf, 0), T.iot[:, 0:C].indirect(ta[:, 0:20]), COPY)
        t2 = run("s", [t1], S.activation, blk(T.tf, 1), blk(T.tf, 0).indirect(ta[:, 0:20]), COPY)
        b2 = run("v", [b1], V.tensor_copy, blk(T.bw, 1), blk(T.bw, 0).indirect(off(7)))
        b3 = run("v", [b2], V.tensor_copy, blk(T.bw, 2), blk(T.bw, 1).indirect(off(6)))
        o2 = conv(blk(T.tf, 1), t2, tb[:, 0:20])
        send(lb[:, 0:20], tb[:, 0:20], "ab", o2)
        t4 = run("s", [t2, o2], S.activation, blk(T.tf, 2), blk(T.tf, 1).indirect(tb[:, 0:20]), COPY)
        ro = conv(blk(T.bw, 2), b3, off(8))
        fd = [run("v", [fw[b]], V.tensor_copy, blk(T.fd, b), blk(T.fw, b)) for b in (0, 1)]
        sg = run("s", [ro, sf[1]], S.activation, T.sg[:], T.sf[:, 0:C].indirect(off(8)), COPY)
        o4 = conv(blk(T.tf, 2), t4, tc[:, 0:20])
        send(lc[:, 0:20], tc[:, 0:20], "ac", o4)
        left += 5 * ne
        if i == 0:
            qv = run("v", [("ldv", 16)], V.quantize_mx, T.qv[:, 0:128], T.sv[:, 0:128], T.vin[:])

        at, ab, ac = [("%s%d" % (k, i), na) for k in ("at", "ab", "ac")]
        zs = [run("s", [at, fw[b]], S.activation, blk(T.tmp, b - 2), blk(T.fw, b).indirect(la[:, 0:20]), COPY) for b in (2, 3)]
        z1 = [run("v", [at, fw[b], fd[b]], V.tensor_tensor, blk(T.z1, b), blk(T.fw, b).indirect(la[:, 0:20]), blk(T.fd, b), A.add) for b in (0, 1)]
        z1 += [run("v", [zs[b - 2]], V.tensor_tensor, blk(T.z1, b), blk(T.tmp, b - 2), T.psa[:, 512 * b:512 * b + C], A.add) for b in (2, 3)]
        d1 = [run("s", [z1[b]], S.activation, blk(T.d1, b), blk(T.z1, b), COPY) for b in range(4)]
        z2 = [run("v", [ab, z1[b], d1[b]], V.tensor_tensor, blk(T.z2, b), blk(T.z1, b).indirect(lb[:, 0:20]), blk(T.d1, b), A.add) for b in range(4)]
        d2 = [run("s", [z2[b]], S.activation, blk(T.d2, b), blk(T.z2, b), COPY) for b in range(4)]
        z3 = [run("v", [ac, z2[b], d2[b]], V.tensor_tensor, T.z3[:, b:1280:4], blk(T.z2, b).indirect(lc[:, 0:20]), blk(T.d2, b), A.add) for b in range(4)]
        tz = [run("v", z3, V.quantize_mx, T.qz[:, H * h:H * h + H], T.sz[:, H * h:H * h + H], T.z3[:, 4 * H * h:4 * H * h + 4 * H]) for h in (0, 1)]

        fbank = [T.psf[:, 512:512 + C], T.psf[:, 1024:1024 + C]]
        ff, fo = [], []
        for b in range(4):
            ff.append(run("t", [qe8] + fo[b - 2:b - 1], TE.matmul_mx, fbank[b % 2], mov(T.qe8, b), mov(T.se8, b), q[:, 0:C], s[:, 0:C], True, True))
            fo.append(run("s", [ff[b]], S.activation, blk(T.fo, b), fbank[b % 2], COPY, scale=8.0))

        hbank = [T.psa[:, 0:H], T.psf[:, 512:512 + H]]
        hh = [run("t", [tz[h], ("ldw", 32), fw[3], fo[2]], TE.matmul_mx, hbank[h], mov(T.wq, 0), mov(T.wsq, 0),
                  T.qz[:, H * h:H * h + H], T.sz[:, H * h:H * h + H], True, True) for h in (0, 1)]
        hh += [run("t", [tz[1]], TE.matmul_mx, T.psa[:, 512 * b:512 * b + C], mov(T.wq, b), mov(T.wsq, b),
                   T.qz[:, 0:C], T.sz[:, 0:C], True, True) for b in (1, 2, 3)]
        hw = [run("s", [hh[h]], S.activation, T.hw[:, H * h:H * h + H], hbank[h], COPY, scale=0.03125) for h in (0, 1)][1:]
        hw += [run("s", [hh[b + 1]], S.activation, blk(T.hw, b), T.psa[:, 512 * b:512 * b + C], COPY, scale=0.03125) for b in (1, 2, 3)]

        a = [run("v", [sg], V.tensor_tensor, T.fl[:, H * h:H * h + H], T.sg[:, H * h:H * h + H], sbank[h], A.is_gt) for h in (0, 1)]
        a = scan(T.fl[:], a)
        e = run("v", [a], V.tensor_scalar, T.ew[:], w20(T.sca), T.thr[:, 0:1], T.inv[:, 0:1], A.is_gt, A.mult)

        tx = []
        for b in range(4):
            tx.append(run("v", [hw[b], fo[b], tt], V.tensor_tensor, T.xt[:, b:1280:4], blk(T.hw, b).indirect(ta[:, 0:20]), blk(T.fo, b), A.add))
            if i == 2 and b == 0:
                e = run("v", [e], V.tensor_tensor, T.ed[:], T.ew[:], T.dw[:], A.mult)
            if i == 2 and b == 1:
                l0 = run("v", [e], V.tensor_tensor, T.l0w[:], T.l0w[:], T.ed[:], A.add)
            if i == 2 and b == 2:
                l1 = run("v", [l0, ss], V.tensor_tensor, T.l1w[:], T.ss[:], T.l0w[:], A.subtract)
                l0 = run("v", [l0], V.tensor_copy, T.l0o[:], T.l0w[:])
                l1 = run("v", [l1], V.tensor_copy, T.l1o[:], T.l1w[:])
                lsd = [run("s", [k_if, t], S.activation, T.lsf[:, C * h:C * h + C], T.iof[:, 0:C].indirect(o[:, 0:20]), COPY)
                       for h, t, o in ((0, l0, T.l0o), (1, l1, T.l1o))]
        tq = quant(T.xt, i + 1, [tx, tx])
        if i < 2:
            e = run("v", [e], V.tensor_tensor, T.ed[:], T.ew[:], T.dw[:], A.mult)
            l0 = run("v", [e], V.tensor_tensor, T.l0w[:], T.l0w[:], T.ed[:], A.add)
            eg = run("v", [e], V.tensor_scalar, T.eg[:], T.ed[:], T.scm[:, 0:1], None, A.mult)

    need("y", *lsd)
    g.sync.dma_start(T.ls[:, :], T.lsf[0:128:16, :]).then_inc(T.sem.sto, 16)
    need("y", *tq)
    g.sync.dma_start(T.oc[:, :], T.q3[:, 0:C].bitcast(dt.uint8)).then_inc(T.sem.sto, 16)
    yy = [run("t", [tq[h], qv, hw[3]], TE.matmul_mx, T.psa[:, 512 * h:512 * h + H], T.qv[:, 0:128], T.sv[:, 0:128],
              T.q3[:, H * h:H * h + H], T.s3[:, H * h:H * h + H], True, True) for h in (0, 1)]
    ya = run("v", [yy[0]], V.tensor_copy, T.yf[:, 0:H], T.psa[:, 0:H])
    yb = run("s", [yy[1]], S.activation, T.yf[:, H:C], T.psa[:, 512:512 + H], COPY)
    need("y", ya)
    g.sync.dma_start(T.y[:, 0:H], T.yf[:, 0:H]).then_inc(T.sem.sto, 16)
    need("s", yb)
    g.scalar.dma_start(T.y[:, H:C], T.yf[:, H:C]).then_inc(T.sem.stc, 16)
    for k in range(4):
        g.sync.dma_start(T.osc[4 * k:4 * k + 4, :], T.s3[32 * k:32 * k + 4, 0:C]).then_inc(T.sem.sto, 16)
    need("g", ("cv", cnt["v"]), ("cs", cnt["s"]), ("ct", cnt["t"]), ("cg", cnt["g"]), ("left", left), ("sto", 112), ("stc", 16))
